import numpy as np
import ml_dtypes


def mxq(x, axis, fmt="e4m3"):
    dtype, down = {"e4m3": (ml_dtypes.float8_e4m3fn, 7), "e5m2": (ml_dtypes.float8_e5m2, 14)}[fmt]
    v = np.moveaxis(np.asarray(x, np.float32).astype(ml_dtypes.bfloat16).astype(np.float64), axis, -1)
    blocks = v.reshape(v.shape[:-1] + (-1, 32))
    amax = np.abs(blocks).max(-1, keepdims=True)
    byte = np.maximum(np.where(amax > 0, np.frexp(amax)[1] - 1 + 127, 0) - down, 1)
    scale = np.exp2(byte - 127.0)
    codes = (blocks / scale).astype(np.float32).astype(dtype).astype(np.float64)
    return np.moveaxis((codes * scale).reshape(v.shape), -1, axis)


WIDE = False


def mx_kscale(k):
    if not WIDE:
        return np.ones(k)
    levels = np.array([10, -10, 5, -5, 0])
    if k % 512:
        return np.exp2(np.random.permutation(np.resize(levels, k // 32))).repeat(32)
    a = np.empty((k // 512, 16))
    for p in range(k // 512):
        a[p, :8] = np.random.permutation(np.resize(levels, 8))
        for g in range(8):
            far = levels[np.abs(levels - a[p, g]) >= 10]
            a[p, g + 8] = far[np.random.randint(len(far))]
    return np.exp2(a.ravel()).repeat(32)


def f64(x):
    return np.asarray(x).astype(np.float64)


def striped(idx):
    return np.tile(idx.reshape(-1, 16).T, (8, 1)).astype(np.uint16)


def unstriped(offs):
    return offs[:16].T.reshape(-1).astype(np.int64)


E2M1 = np.array([0.0, 0.5, 1.0, 1.5, 2.0, 3.0, 4.0, 6.0, -0.0, -0.5, -1.0, -1.5, -2.0, -3.0, -4.0, -6.0])


def pack_weight(w, fmt):
    k, n = w.shape
    w = f64(np.asarray(w, np.float32).astype(ml_dtypes.bfloat16)).reshape(k // 32, 32, n)
    amax = np.abs(w).max(1)
    if fmt == "e4m3":
        byte = np.frexp(amax)[1] - 1 + 127 - 7
    else:
        mant, ex = np.frexp(amax / 6.0)
        byte = np.where(mant > 0.5, ex, ex - 1) + 127
    byte = np.clip(np.where(amax > 0, byte, 1), 1, 254)
    scaled = (w * np.exp2(127.0 - byte)[:, None, :]).reshape(k, n).astype(np.float32)
    by_word = np.ascontiguousarray(scaled.reshape(k // 512, 128, 4, n).transpose(0, 1, 3, 2))
    if fmt == "e4m3":
        words = by_word.astype(ml_dtypes.float8_e4m3fn).view(np.uint8)
    else:
        c = by_word.astype(ml_dtypes.float4_e2m1fn).view(np.uint8) & 0xF
        words = (c[..., 0::2] | (c[..., 1::2] << 4)).reshape(k // 512, 128, 2 * n)
    return np.ascontiguousarray(words), np.ascontiguousarray(byte.astype(np.uint8).reshape(k // 512, 16, n))


def unpack_weight(words, scales, fmt):
    g, _, n = scales.shape
    words = np.ascontiguousarray(words).reshape(g, 128, n, -1)
    if fmt == "e4m3":
        vals = words.view(ml_dtypes.float8_e4m3fn).astype(np.float64)
    else:
        nib = np.empty((g, 128, n, 4), np.uint8)
        nib[..., 0::2] = words & 0xF
        nib[..., 1::2] = words >> 4
        vals = E2M1[nib]
    vals = vals * np.repeat(np.exp2(scales.astype(np.float64) - 127.0), 8, axis=1)[..., None]
    return vals.transpose(0, 1, 3, 2).reshape(g * 512, n)


def gelu(v):
    return 0.5 * v * (1.0 + np.tanh(np.sqrt(2.0 / np.pi) * (v + 0.044715 * v**3)))


def bf(x):
    return np.asarray(x, np.float32).astype(ml_dtypes.bfloat16)

def planes(Y):
    n, m = Y.shape
    b = f64(bf(Y)).reshape(n // 32, 32, m)
    amax = np.abs(b).max(1)
    byte = np.clip(np.where(amax > 0, np.frexp(amax)[1] - 1 + 127 - 7, 1), 1, 254)
    codes = (b * np.exp2(127.0 - byte)[:, None, :]).reshape(n, m).astype(np.float32).astype(ml_dtypes.float8_e4m3fn).view(np.uint8)
    words = codes.reshape(n // 512, 128, 4, m).transpose(0, 1, 3, 2)
    return np.ascontiguousarray(words), np.ascontiguousarray(byte.astype(np.uint8).reshape(n // 512, 16, m))


K, K2, H, N, T, T2, S = 1024, 512, 1024, 512, 4096, 2048, 1024

def setup_inputs():
    n = np.random.standard_normal
    s = mx_kscale(K)[:, None]
    s2 = mx_kscale(K2)[:, None]
    u = mx_kscale(H)[:, None]
    e = np.exp(0.8 * n(N))
    tab_words, tab_scales = pack_weight(n((K, T)) * s, "e4m3")
    tab2_words, tab2_scales = pack_weight(n((K2, T2)) * s2, "e4m3")
    w2_words, w2_scales = pack_weight(0.7 * n((K2, H)) / np.sqrt(K2) / s2 * u.T, "e2m1")
    return {
        "tab_words": tab_words, "tab_scales": tab_scales,
        "tab2_words": tab2_words, "tab2_scales": tab2_scales,
        "offs": striped(np.random.permutation(T)[:S]),
        "offs2": striped(np.random.permutation(T2)[:S]),
        "w1": (0.5 * n((K, H)) / np.sqrt(K) / s).astype(np.float32),
        "w2_words": w2_words, "w2_scales": w2_scales,
        "x": (n((H, S)) * u).astype(np.float32),
        "w3": (n((H, N)) / np.sqrt(H) / u * e[None, :]).astype(np.float32),
        "b3": (0.3 * n(N) * e).astype(np.float32),
    }

def reference(tab_words, tab_scales, tab2_words, tab2_scales, offs, offs2, w1, w2_words, w2_scales, x, w3, b3):
    v = unpack_weight(tab_words, tab_scales, "e4m3")[:, unstriped(offs)]
    v2 = unpack_weight(tab2_words, tab2_scales, "e4m3")[:, unstriped(offs2)]
    w2 = unpack_weight(w2_words, w2_scales, "e2m1")
    a = mxq(f64(w1), 0, "e4m3").T @ v
    b = w2.T @ v2
    h = f64(x) * (1.0 + a) + b
    y = (mxq(f64(w3), 0, "e4m3").T @ mxq(h, 0, "e4m3")) + f64(b3)[:, None]
    words, scales = planes(y)
    return y, words, scales

@@ -1,0 +1,283 @@
+from contextlib import ExitStack
+
+import concourse.mybir as mybir
+
+K, K2, H, N, T, T2, S = 1024, 512, 1024, 512, 4096, 2048, 1024
+FLOPS = 2 * S * (K * H + K2 * H + H * N)
+
+F32 = mybir.dt.float32
+BF16 = mybir.dt.bfloat16
+I32 = mybir.dt.int32
+U32 = mybir.dt.uint32
+U16 = mybir.dt.uint16
+U8 = mybir.dt.uint8
+E4M3 = mybir.dt.float8_e4m3fn_x4
+E2M1 = mybir.dt.float4_e2m1fn_x4
+ADD = mybir.AluOpType.add
+MULT = mybir.AluOpType.mult
+IDENTITY = mybir.ActivationFunctionType.Identity
+
+P = 128
+PACK = 4
+PASS = P * PACK
+BLOCK = 128
+BLOCKS = S // BLOCK
+HALF = S // 2
+X_PIECES = [[(0, 256), (256, 512), (512, 1024)], [(0, 256), (256, 512), (512, 768), (768, 1024)]]
+STORE = 256
+SHARED = []
+
+
+def tile_list_style_modulated_decoder_kernel(
+    tc, tab_words, tab_scales, tab2_words, tab2_scales, offs, offs2, w1, w2_words, w2_scales, x, w3, b3,
+    out_0, out_1, out_2,
+):
+    nc = tc.nc
+    with ExitStack() as ctx:
+        keep = ctx.enter_context(tc.tile_pool(name="keep", bufs=1))
+        ring = ctx.enter_context(tc.tile_pool(name="ring", bufs=3))
+        psum = ctx.enter_context(tc.psum_pool(name="psum", bufs=3))
+        psum_y = ctx.enter_context(tc.psum_pool(name="psum_y", bufs=2))
+
+        def held(name, shape, dtype):
+            return keep.tile(shape, dtype, name=name, align_bytes=64)
+
+        list1 = held("list1", [P, S // 16], U16)
+        list2 = held("list2", [P, S // 16], U16)
+        nc.sync.dma_start(list2[:], offs2)
+        nc.sync.dma_start(list1[:], offs)
+
+        w2_plane_raw = held("w2_plane_raw", [P, H], U8)
+        tab2_plane = held("tab2_plane", [P, T2], U8)
+        tab_plane = held("tab_plane", [P, T], U8)
+        for plane in (w2_plane_raw, tab2_plane, tab_plane):
+            nc.vector.memset(plane[:].bitcast(I32), 0)
+        def load_plane(plane, scales, first_row):
+            rows = 4 * scales.shape[0]
+            for q in range(4):
+                nc.sync.dma_start(
+                    plane[32 * q + first_row : 32 * q + first_row + rows, :].bitcast(I32),
+                    scales[:, 4 * q : 4 * q + 4, :].bitcast(I32),
+                )
+
+        def load_words(name, words, width):
+            tile = held(name, [P, width], U32)
+            nc.sync.dma_start(tile[:].bitcast(I32), words.rearrange("p n t -> p (n t)").bitcast(I32))
+            return tile
+
+        def load_rows(name, rows):
+            tile = held(name, [P, PACK, rows.shape[1]], F32)
+            nc.sync.dma_start(tile[:], rows.rearrange("(p t) c -> p t c", t=PACK))
+            return tile
+
+        def load_w1(a, g):
+            return load_rows("w1_raw_%d_%d" % (a, g), w1[a * PASS : (a + 1) * PASS, g * PASS : (g + 1) * PASS])
+
+        def load_x(g, piece):
+            lo, hi = piece
+            return load_rows("x_%d_%d" % (g, lo), x[g * PASS : (g + 1) * PASS, lo:hi])
+
+        w2_raw = held("w2_raw", [P, 2 * H], U8)
+        nc.sync.dma_start(w2_raw[:].bitcast(I32), w2_words[0].bitcast(I32))
+        tab2 = load_words("tab2", tab2_words[0], T2)
+        load_plane(w2_plane_raw, w2_scales, 0)
+        w1_raw = {}
+        x_sb = {}
+        w1_raw[0, 0] = load_w1(0, 0)
+        load_plane(tab2_plane, tab2_scales, 0)
+        tab = [load_words("tab_0", tab_words[0], T)]
+        load_plane(tab_plane, tab_scales, 4)
+        w1_raw[1, 0] = load_w1(1, 0)
+        tab.append(load_words("tab_1", tab_words[1], T))
+        bias = held("bias", [P, PACK], F32)
+        nc.sync.dma_start(bias[:], b3.rearrange("(p t) -> p t", t=PACK))
+        for piece in X_PIECES[0]:
+            x_sb[0, piece] = load_x(0, piece)
+        w1_raw[0, 1] = load_w1(0, 1)
+        w1_raw[1, 1] = load_w1(1, 1)
+        x_sb[1, X_PIECES[1][0]] = load_x(1, X_PIECES[1][0])
+        w3_raw = [load_rows("w3_raw_%d" % g, w3[g * PASS : (g + 1) * PASS, :]) for g in range(2)]
+        for piece in X_PIECES[1][1:]:
+            x_sb[1, piece] = load_x(1, piece)
+
+        def x_block(g, jb):
+            lo = jb * BLOCK
+            for piece in X_PIECES[g]:
+                if piece[0] <= lo < piece[1]:
+                    return x_sb[g, piece][:, :, lo - piece[0] : lo - piece[0] + BLOCK]
+
+        def gather(name, window, offsets, dtype, parts):
+            width = S // parts
+            tiles = []
+            for h in range(parts):
+                picked = held("%s_%d" % (name, h), [P, width], dtype)
+                nc.vector.tensor_copy(picked[:], window[:].indirect(offsets[:, h * width // 16 : (h + 1) * width // 16]))
+                tiles.append(picked)
+            return tiles
+
+        def block_of(tiles, jb, first_row=0):
+            width = S // len(tiles)
+            lo = jb * BLOCK % width
+            return tiles[jb * BLOCK // width][first_row:P, lo : lo + BLOCK]
+
+        def round_weight(raw):
+            dealt = ring.tile([P, PACK * PASS], BF16, name="dealt", align_bytes=64, bufs=4)
+            nc.scalar.copy(
+                dealt[:].rearrange("p (t m j) -> p m j t", t=PACK, j=PACK),
+                raw[:].rearrange("p j (m t) -> p m j t", t=PACK),
+            )
+            return dealt
+
+        def quantise(name, rounded, width, calls=1):
+            codes = held(name + "_codes", [P, width], U32)
+            plane = held(name + "_plane", [P, width], U8)
+            step = width // calls
+            for lo in range(0, width, step):
+                nc.vector.quantize_mx(
+                    codes[:, lo : lo + step].bitcast(E4M3), plane[:, lo : lo + step], rounded[:, PACK * lo : PACK * (lo + step)]
+                )
+            return codes, plane
+
+        w2_dealt = held("w2_dealt", [P, 2 * H], U8)
+        nc.vector.tensor_copy(
+            w2_dealt[:].bitcast(U16).rearrange("p (g t m) -> p g t m", g=2, t=PACK),
+            w2_raw[:].bitcast(U16).rearrange("p (g m t) -> p g t m", g=2, t=PACK),
+        )
+        v2_words = gather("v2_words", tab2, list2, U32, 1)
+        w2_plane = held("w2_plane", [P, H], U8)
+        nc.vector.tensor_copy(
+            w2_plane[:].rearrange("p (g t m) -> p g t m", g=2, t=PACK),
+            w2_plane_raw[:].rearrange("p (g m t) -> p g t m", g=2, t=PACK),
+        )
+        w1_q = {}
+        w1_q[0, 0] = quantise("w1_0_0", round_weight(w1_raw[0, 0]), PASS)
+        v2_plane = gather("v2_plane", tab2_plane, list2, U8, 1)
+        v_words = [gather("v_words_0", tab[0], list1, U32, 1)]
+        v_plane = gather("v_plane", tab_plane, list1, U8, 1)
+        w1_q[1, 0] = quantise("w1_1_0", round_weight(w1_raw[1, 0]), PASS)
+        v_words.append(gather("v_words_1", tab[1], list1, U32, 2))
+
+        def style(g, jb):
+            a_bank = psum.tile([P, PACK, BLOCK], F32, name="a_bank")
+            for a in range(2):
+                for t in range(PACK):
+                    codes, plane = w1_q[a, g]
+                    cols = slice(t * P, (t + 1) * P)
+                    nc.tensor.matmul_mx(
+                        a_bank[:, t, :],
+                        lhsT=codes[:, cols].bitcast(E4M3), lhsT_scale=plane[:, cols],
+                        rhs=block_of(v_words[a], jb).bitcast(E4M3), rhs_scale=block_of(v_plane, jb, 4 + 4 * a),
+                        start=(a == 0 and t == 0), stop=(a == 1 and t == PACK - 1),
+                    )
+            scaled = ring.tile([P, PACK, BLOCK], F32, name="scaled", align_bytes=64)
+            nc.vector.scalar_tensor_tensor(scaled[:], a_bank[:], 1.0, x_block(g, jb), ADD, MULT)
+            return scaled
+
+        def shift_product(g, jb):
+            b_bank = psum.tile([P, PACK, BLOCK], F32, name="b_bank")
+            for t in range(PACK):
+                lo = g * PASS + t * P
+                nc.tensor.matmul_mx(
+                    b_bank[:, t, :],
+                    lhsT=w2_dealt[:, 2 * lo : 2 * (lo + P)].bitcast(E2M1), lhsT_scale=w2_plane[:, lo : lo + P],
+                    rhs=block_of(v2_words, jb).bitcast(E4M3), rhs_scale=block_of(v2_plane, jb),
+                    start=True, stop=True,
+                )
+            return b_bank
+
+        units = [(g, jb) for g in range(2) for jb in range(BLOCKS)]
+        parked = {}
+        for u in SHARED:
+            parked[u] = held("parked_%d" % u, [P, BLOCK, PACK], F32)
+            nc.scalar.copy(parked[u][:], shift_product(*units[u])[:].rearrange("p t j -> p j t"))
+
+        def shift(u, scaled, h_rounded):
+            if u in parked:
+                nc.gpsimd.tensor_tensor(
+                    h_rounded.rearrange("p (j t) -> p j t", t=PACK), parked[u][:],
+                    scaled[:].rearrange("p t j -> p j t"), ADD,
+                )
+            else:
+                nc.vector.tensor_tensor(
+                    h_rounded.rearrange("p (c i t) -> p c t i", i=4, t=PACK),
+                    shift_product(*units[u])[:].rearrange("p t (c i) -> p c t i", i=4),
+                    scaled[:].rearrange("p t (c i) -> p c t i", i=4),
+                    ADD,
+                )
+
+        y_plane = held("y_plane", [P, S], U8)
+        y_sb = [held("w1_raw_%d_0" % s, [P, PACK, HALF], F32) for s in range(2)]
+        y_codes = [held("y_codes_%d" % s, [P, STORE], U32) for s in range(S // STORE)]
+        out_rows = out_0.rearrange("(p t) j -> p t j", t=PACK)
+        out_words = out_1[0].rearrange("p m t -> p (m t)").bitcast(I32)
+        h_q = {}
+        w3_q = []
+
+        def decode(jb):
+            y_bank = psum_y.tile([P, PACK, BLOCK], F32, name="y_bank")
+            for t in range(PACK):
+                for g in range(2):
+                    codes, plane = w3_q[g]
+                    h_codes, h_plane = h_q[g, jb // 2]
+                    pair_cols = slice(jb % 2 * BLOCK, (jb % 2 + 1) * BLOCK)
+                    cols = slice(t * P, (t + 1) * P)
+                    nc.tensor.matmul_mx(
+                        y_bank[:, t, :],
+                        lhsT=codes[:, cols].bitcast(E4M3), lhsT_scale=plane[:, cols],
+                        rhs=h_codes[:, pair_cols].bitcast(E4M3), rhs_scale=h_plane[:, pair_cols],
+                        start=(g == 0), stop=(g == 1),
+                    )
+            half, at = divmod(jb * BLOCK, HALF)
+            y_block = y_sb[half][:, :, at : at + BLOCK]
+            for t in range(PACK):
+                nc.scalar.activation(y_block[:, t, :], y_bank[:, t, :], IDENTITY, bias=bias[:, t : t + 1])
+            if (at + BLOCK) % STORE == 0:
+                done = (jb + 1) * BLOCK
+                nc.sync.dma_start(out_rows[:, :, done - STORE : done], y_sb[half][:, :, at + BLOCK - STORE : at + BLOCK])
+            y_rounded = ring.tile([P, PACK * BLOCK], BF16, name="y_rounded", align_bytes=64, bufs=4)
+            copy = nc.vector.tensor_copy if jb == BLOCKS - 1 else nc.scalar.copy
+            copy(
+                y_rounded[:].rearrange("p (c i t) -> p c t i", i=4, t=PACK),
+                y_block.rearrange("p t (c i) -> p c t i", i=4),
+            )
+            return y_rounded
+
+        def pack_y(jb, y_rounded):
+            s, lo = divmod(jb * BLOCK, STORE)
+            nc.vector.quantize_mx(
+                y_codes[s][:, lo : lo + BLOCK].bitcast(E4M3), y_plane[:, jb * BLOCK : (jb + 1) * BLOCK], y_rounded[:]
+            )
+            if lo + BLOCK == STORE:
+                nc.sync.dma_start(out_words[:, s * STORE : (s + 1) * STORE], y_codes[s][:].bitcast(I32))
+
+        pairs = len(units) // 2
+        rounded, decoded = {}, {}
+        for pair in range(pairs + 2):
+            if pair < pairs:
+                first, second = 2 * pair, 2 * pair + 1
+                rounded[pair] = ring.tile([P, 2 * PACK * BLOCK], BF16, name="h_rounded", align_bytes=64)
+                scaled_first = style(*units[first])
+                if first in parked:
+                    shift(first, scaled_first, rounded[pair][:, : PACK * BLOCK])
+                scaled_second = style(*units[second])
+                if first not in parked:
+                    shift(first, scaled_first, rounded[pair][:, : PACK * BLOCK])
+                shift(second, scaled_second, rounded[pair][:, PACK * BLOCK :])
+            if 0 <= pair - 1 < pairs:
+                g, jb = units[2 * (pair - 1)]
+                h_q[g, jb // 2] = quantise("h_%d_%d" % (g, jb), rounded[pair - 1], 2 * BLOCK, 2 if pair == pairs else 1)
+            if pair in (2, 3):
+                w1_q[pair - 2, 1] = quantise("w1_%d_1" % (pair - 2), round_weight(w1_raw[pair - 2, 1]), PASS)
+            if pair in (4, 5):
+                w3_q.append(quantise("w3_%d" % (pair - 4), round_weight(w3_raw[pair - 4]), N))
+            for jb in sorted(decoded):
+                pack_y(jb, decoded[jb])
+            decoded = {}
+            if pair - 1 >= pairs // 2:
+                first = 2 * (pair - 1) - BLOCKS
+                for jb in (first, first + 1):
+                    if jb < BLOCKS:
+                        decoded[jb] = decode(jb)
+
+        for q in range(4):
+            nc.sync.dma_start(out_2[0, 4 * q : 4 * q + 4, :].bitcast(I32), y_plane[32 * q : 32 * q + 4, :].bitcast(I32))

@@ -23,8 +23,8 @@ PASS = P * PACK
 BLOCK = 128
 BLOCKS = S // BLOCK
 HALF = S // 2
-X_PIECES = [[(0, 256), (256, 512), (512, 1024)], [(0, 256), (256, 512), (512, 768), (768, 1024)]]
-STORE = 256
+X_PIECES = [[(0, 512), (512, 1024)], [(0, 512), (512, 1024)]]
+STORES = [(0, 512), (512, 768), (768, 1024)]
 SHARED = []
 
 
@@ -95,10 +95,10 @@ def tile_list_style_modulated_decoder_kernel(
             x_sb[0, piece] = load_x(0, piece)
         w1_raw[0, 1] = load_w1(0, 1)
         w1_raw[1, 1] = load_w1(1, 1)
-        x_sb[1, X_PIECES[1][0]] = load_x(1, X_PIECES[1][0])
-        w3_raw = [load_rows("w3_raw_%d" % g, w3[g * PASS : (g + 1) * PASS, :]) for g in range(2)]
-        for piece in X_PIECES[1][1:]:
-            x_sb[1, piece] = load_x(1, piece)
+        w3_raw = []
+        for g in range(2):
+            w3_raw.append(load_rows("w3_raw_%d" % g, w3[g * PASS : (g + 1) * PASS, :]))
+            x_sb[1, X_PIECES[1][g]] = load_x(1, X_PIECES[1][g])
 
         def x_block(g, jb):
             lo = jb * BLOCK
@@ -123,8 +123,8 @@ def tile_list_style_modulated_decoder_kernel(
         def round_weight(raw):
             dealt = ring.tile([P, PACK * PASS], BF16, name="dealt", align_bytes=64, bufs=4)
             nc.scalar.copy(
-                dealt[:].rearrange("p (t m j) -> p m j t", t=PACK, j=PACK),
-                raw[:].rearrange("p j (m t) -> p m j t", t=PACK),
+                dealt[:].rearrange("p (u e m j) -> p u m j e", u=2, e=2, j=PACK),
+                raw[:].rearrange("p j (m u e) -> p u m j e", u=2, e=2),
             )
             return dealt
 
@@ -199,15 +199,15 @@ def tile_list_style_modulated_decoder_kernel(
                 )
             else:
                 nc.vector.tensor_tensor(
-                    h_rounded.rearrange("p (c i t) -> p c t i", i=4, t=PACK),
-                    shift_product(*units[u])[:].rearrange("p t (c i) -> p c t i", i=4),
-                    scaled[:].rearrange("p t (c i) -> p c t i", i=4),
+                    h_rounded.rearrange("p (c i t) -> p c t i", i=2, t=PACK),
+                    shift_product(*units[u])[:].rearrange("p t (c i) -> p c t i", i=2),
+                    scaled[:].rearrange("p t (c i) -> p c t i", i=2),
                     ADD,
                 )
 
         y_plane = held("y_plane", [P, S], U8)
         y_sb = [held("w1_raw_%d_0" % s, [P, PACK, HALF], F32) for s in range(2)]
-        y_codes = [held("y_codes_%d" % s, [P, STORE], U32) for s in range(S // STORE)]
+        y_codes = held("y_codes", [P, S], U32)
         out_rows = out_0.rearrange("(p t) j -> p t j", t=PACK)
         out_words = out_1[0].rearrange("p m t -> p (m t)").bitcast(I32)
         h_q = {}
@@ -231,24 +231,23 @@ def tile_list_style_modulated_decoder_kernel(
             y_block = y_sb[half][:, :, at : at + BLOCK]
             for t in range(PACK):
                 nc.scalar.activation(y_block[:, t, :], y_bank[:, t, :], IDENTITY, bias=bias[:, t : t + 1])
-            if (at + BLOCK) % STORE == 0:
-                done = (jb + 1) * BLOCK
-                nc.sync.dma_start(out_rows[:, :, done - STORE : done], y_sb[half][:, :, at + BLOCK - STORE : at + BLOCK])
+            for lo, hi in STORES:
+                if hi == (jb + 1) * BLOCK:
+                    nc.sync.dma_start(out_rows[:, :, lo:hi], y_sb[half][:, :, lo - half * HALF : hi - half * HALF])
             y_rounded = ring.tile([P, PACK * BLOCK], BF16, name="y_rounded", align_bytes=64, bufs=4)
             copy = nc.vector.tensor_copy if jb == BLOCKS - 1 else nc.scalar.copy
             copy(
-                y_rounded[:].rearrange("p (c i t) -> p c t i", i=4, t=PACK),
-                y_block.rearrange("p t (c i) -> p c t i", i=4),
+                y_rounded[:].rearrange("p (c i t) -> p c t i", i=2, t=PACK),
+                y_block.rearrange("p t (c i) -> p c t i", i=2),
             )
             return y_rounded
 
         def pack_y(jb, y_rounded):
-            s, lo = divmod(jb * BLOCK, STORE)
-            nc.vector.quantize_mx(
-                y_codes[s][:, lo : lo + BLOCK].bitcast(E4M3), y_plane[:, jb * BLOCK : (jb + 1) * BLOCK], y_rounded[:]
-            )
-            if lo + BLOCK == STORE:
-                nc.sync.dma_start(out_words[:, s * STORE : (s + 1) * STORE], y_codes[s][:].bitcast(I32))
+            cols = slice(jb * BLOCK, (jb + 1) * BLOCK)
+            nc.vector.quantize_mx(y_codes[:, cols].bitcast(E4M3), y_plane[:, cols], y_rounded[:])
+            for lo, hi in STORES:
+                if hi == cols.stop:
+                    nc.sync.dma_start(out_words[:, lo:hi], y_codes[:, lo:hi].bitcast(I32))
 
         pairs = len(units) // 2
         rounded, decoded = {}, {}

@@ -23,6 +23,7 @@ PASS = P * PACK
 BLOCK = 128
 BLOCKS = S // BLOCK
 HALF = S // 2
+PAIR = 2 * BLOCK
 X_PIECES = [[(0, 512), (512, 1024)], [(0, 512), (512, 1024)]]
 STORES = [(0, 512), (512, 768), (768, 1024)]
 SHARED = []
@@ -50,15 +51,16 @@ def tile_list_style_modulated_decoder_kernel(
         w2_plane_raw = held("w2_plane_raw", [P, H], U8)
         tab2_plane = held("tab2_plane", [P, T2], U8)
         tab_plane = held("tab_plane", [P, T], U8)
-        for plane in (w2_plane_raw, tab2_plane, tab_plane):
+        for plane in (tab_plane, w2_plane_raw, tab2_plane):
             nc.vector.memset(plane[:].bitcast(I32), 0)
-        def load_plane(plane, scales, first_row):
-            rows = 4 * scales.shape[0]
-            for q in range(4):
-                nc.sync.dma_start(
-                    plane[32 * q + first_row : 32 * q + first_row + rows, :].bitcast(I32),
-                    scales[:, 4 * q : 4 * q + 4, :].bitcast(I32),
-                )
+        for q in range(4):
+            nc.gpsimd.dma_start(
+                tab_plane[32 * q + 4 : 32 * q + 12, :].bitcast(I32), tab_scales[:, 4 * q : 4 * q + 4, :].bitcast(I32)
+            )
+
+        def load_plane(plane, scales):
+            for r in range(4):
+                nc.sync.dma_start(plane[r:P:32, :].bitcast(I32), scales[0, r:16:4, :].bitcast(I32))
 
         def load_words(name, words, width):
             tile = held(name, [P, width], U32)
@@ -80,13 +82,12 @@ def tile_list_style_modulated_decoder_kernel(
         w2_raw = held("w2_raw", [P, 2 * H], U8)
         nc.sync.dma_start(w2_raw[:].bitcast(I32), w2_words[0].bitcast(I32))
         tab2 = load_words("tab2", tab2_words[0], T2)
-        load_plane(w2_plane_raw, w2_scales, 0)
+        load_plane(w2_plane_raw, w2_scales)
         w1_raw = {}
         x_sb = {}
         w1_raw[0, 0] = load_w1(0, 0)
-        load_plane(tab2_plane, tab2_scales, 0)
+        load_plane(tab2_plane, tab2_scales)
         tab = [load_words("tab_0", tab_words[0], T)]
-        load_plane(tab_plane, tab_scales, 4)
         w1_raw[1, 0] = load_w1(1, 0)
         tab.append(load_words("tab_1", tab_words[1], T))
         bias = held("bias", [P, PACK], F32)
@@ -100,11 +101,9 @@ def tile_list_style_modulated_decoder_kernel(
             w3_raw.append(load_rows("w3_raw_%d" % g, w3[g * PASS : (g + 1) * PASS, :]))
             x_sb[1, X_PIECES[1][g]] = load_x(1, X_PIECES[1][g])
 
-        def x_block(g, jb):
-            lo = jb * BLOCK
-            for piece in X_PIECES[g]:
-                if piece[0] <= lo < piece[1]:
-                    return x_sb[g, piece][:, :, lo - piece[0] : lo - piece[0] + BLOCK]
+        def x_block(g, rows, lo, width):
+            piece = X_PIECES[g][lo // HALF]
+            return x_sb[g, piece][:, rows, lo - piece[0] : lo - piece[0] + width]
 
         def gather(name, window, offsets, dtype, parts):
             width = S // parts
@@ -115,10 +114,9 @@ def tile_list_style_modulated_decoder_kernel(
                 tiles.append(picked)
             return tiles
 
-        def block_of(tiles, jb, first_row=0):
+        def columns(tiles, lo, count, first_row=0):
             width = S // len(tiles)
-            lo = jb * BLOCK % width
-            return tiles[jb * BLOCK // width][first_row:P, lo : lo + BLOCK]
+            return tiles[lo // width][first_row:P, lo % width : lo % width + count]
 
         def round_weight(raw):
             dealt = ring.tile([P, PACK * PASS], BF16, name="dealt", align_bytes=64, bufs=4)
@@ -157,21 +155,20 @@ def tile_list_style_modulated_decoder_kernel(
         w1_q[1, 0] = quantise("w1_1_0", round_weight(w1_raw[1, 0]), PASS)
         v_words.append(gather("v_words_1", tab[1], list1, U32, 2))
 
-        def style(g, jb):
-            a_bank = psum.tile([P, PACK, BLOCK], F32, name="a_bank")
+        def scale_rows(g, lo, u, scaled):
+            a_bank = psum.tile([P, 2, PAIR], F32, name="a_bank")
             for a in range(2):
-                for t in range(PACK):
-                    codes, plane = w1_q[a, g]
-                    cols = slice(t * P, (t + 1) * P)
+                codes, plane = w1_q[a, g]
+                for e in range(2):
+                    cols = slice((2 * u + e) * P, (2 * u + e + 1) * P)
                     nc.tensor.matmul_mx(
-                        a_bank[:, t, :],
+                        a_bank[:, e, :],
                         lhsT=codes[:, cols].bitcast(E4M3), lhsT_scale=plane[:, cols],
-                        rhs=block_of(v_words[a], jb).bitcast(E4M3), rhs_scale=block_of(v_plane, jb, 4 + 4 * a),
-                        start=(a == 0 and t == 0), stop=(a == 1 and t == PACK - 1),
+                        rhs=columns(v_words[a], lo, PAIR).bitcast(E4M3), rhs_scale=columns(v_plane, lo, PAIR, 4 + 4 * a),
+                        start=(a == 0 and e == 0), stop=(a == 1 and e == 1),
                     )
-            scaled = ring.tile([P, PACK, BLOCK], F32, name="scaled", align_bytes=64)
-            nc.vector.scalar_tensor_tensor(scaled[:], a_bank[:], 1.0, x_block(g, jb), ADD, MULT)
-            return scaled
+            rows = slice(2 * u, 2 * u + 2)
+            nc.vector.scalar_tensor_tensor(scaled[:, rows, :], a_bank[:], 1.0, x_block(g, rows, lo, PAIR), ADD, MULT)
 
         def shift_product(g, jb):
             b_bank = psum.tile([P, PACK, BLOCK], F32, name="b_bank")
@@ -180,7 +177,7 @@ def tile_list_style_modulated_decoder_kernel(
                 nc.tensor.matmul_mx(
                     b_bank[:, t, :],
                     lhsT=w2_dealt[:, 2 * lo : 2 * (lo + P)].bitcast(E2M1), lhsT_scale=w2_plane[:, lo : lo + P],
-                    rhs=block_of(v2_words, jb).bitcast(E4M3), rhs_scale=block_of(v2_plane, jb),
+                    rhs=columns(v2_words, jb * BLOCK, BLOCK).bitcast(E4M3), rhs_scale=columns(v2_plane, jb * BLOCK, BLOCK),
                     start=True, stop=True,
                 )
             return b_bank
@@ -192,16 +189,19 @@ def tile_list_style_modulated_decoder_kernel(
             nc.scalar.copy(parked[u][:], shift_product(*units[u])[:].rearrange("p t j -> p j t"))
 
         def shift(u, scaled, h_rounded):
+            at = u % 2 * BLOCK
+            scaled_block = scaled[:, :, at : at + BLOCK]
+            h_block = h_rounded[:, PACK * at : PACK * (at + BLOCK)]
             if u in parked:
                 nc.gpsimd.tensor_tensor(
-                    h_rounded.rearrange("p (j t) -> p j t", t=PACK), parked[u][:],
-                    scaled[:].rearrange("p t j -> p j t"), ADD,
+                    h_block.rearrange("p (j t) -> p j t", t=PACK), parked[u][:],
+                    scaled_block.rearrange("p t j -> p j t"), ADD,
                 )
             else:
                 nc.vector.tensor_tensor(
-                    h_rounded.rearrange("p (c i t) -> p c t i", i=2, t=PACK),
+                    h_block.rearrange("p (c i t) -> p c t i", i=2, t=PACK),
                     shift_product(*units[u])[:].rearrange("p t (c i) -> p c t i", i=2),
-                    scaled[:].rearrange("p t (c i) -> p c t i", i=2),
+                    scaled_block.rearrange("p t (c i) -> p c t i", i=2),
                     ADD,
                 )
 
@@ -213,70 +213,76 @@ def tile_list_style_modulated_decoder_kernel(
         h_q = {}
         w3_q = []
 
-        def decode(jb):
-            y_bank = psum_y.tile([P, PACK, BLOCK], F32, name="y_bank")
-            for t in range(PACK):
-                for g in range(2):
-                    codes, plane = w3_q[g]
-                    h_codes, h_plane = h_q[g, jb // 2]
-                    pair_cols = slice(jb % 2 * BLOCK, (jb % 2 + 1) * BLOCK)
-                    cols = slice(t * P, (t + 1) * P)
-                    nc.tensor.matmul_mx(
-                        y_bank[:, t, :],
-                        lhsT=codes[:, cols].bitcast(E4M3), lhsT_scale=plane[:, cols],
-                        rhs=h_codes[:, pair_cols].bitcast(E4M3), rhs_scale=h_plane[:, pair_cols],
-                        start=(g == 0), stop=(g == 1),
-                    )
-            half, at = divmod(jb * BLOCK, HALF)
-            y_block = y_sb[half][:, :, at : at + BLOCK]
-            for t in range(PACK):
-                nc.scalar.activation(y_block[:, t, :], y_bank[:, t, :], IDENTITY, bias=bias[:, t : t + 1])
-            for lo, hi in STORES:
-                if hi == (jb + 1) * BLOCK:
-                    nc.sync.dma_start(out_rows[:, :, lo:hi], y_sb[half][:, :, lo - half * HALF : hi - half * HALF])
-            y_rounded = ring.tile([P, PACK * BLOCK], BF16, name="y_rounded", align_bytes=64, bufs=4)
-            copy = nc.vector.tensor_copy if jb == BLOCKS - 1 else nc.scalar.copy
+        def decode(lo, width):
+            half, at = divmod(lo, HALF)
+            y_block = y_sb[half][:, :, at : at + width]
+            slots = PASS // width
+            for first in range(0, PACK, slots):
+                y_bank = psum_y.tile([P, slots, width], F32, name="y_bank")
+                for e in range(slots):
+                    cols = slice((first + e) * P, (first + e + 1) * P)
+                    for g in range(2):
+                        codes, plane = w3_q[g]
+                        h_codes, h_plane = h_q[g, lo // PAIR]
+                        h_cols = slice(lo % PAIR, lo % PAIR + width)
+                        nc.tensor.matmul_mx(
+                            y_bank[:, e, :],
+                            lhsT=codes[:, cols].bitcast(E4M3), lhsT_scale=plane[:, cols],
+                            rhs=h_codes[:, h_cols].bitcast(E4M3), rhs_scale=h_plane[:, h_cols],
+                            start=(g == 0), stop=(g == 1),
+                        )
+                for e in range(slots):
+                    t = first + e
+                    nc.scalar.activation(y_block[:, t, :], y_bank[:, e, :], IDENTITY, bias=bias[:, t : t + 1])
+            for start, stop in STORES:
+                if stop == lo + width:
+                    nc.sync.dma_start(out_rows[:, :, start:stop], y_sb[half][:, :, start - half * HALF : stop - half * HALF])
+            y_rounded = ring.tile([P, PACK * PAIR], BF16, name="y_rounded", align_bytes=64)
+            copy = nc.vector.tensor_copy if lo + width == S else nc.scalar.copy
             copy(
-                y_rounded[:].rearrange("p (c i t) -> p c t i", i=2, t=PACK),
+                y_rounded[:, : PACK * width].rearrange("p (c i t) -> p c t i", i=2, t=PACK),
                 y_block.rearrange("p t (c i) -> p c t i", i=2),
             )
-            return y_rounded
+            return lo, width, y_rounded
 
-        def pack_y(jb, y_rounded):
-            cols = slice(jb * BLOCK, (jb + 1) * BLOCK)
-            nc.vector.quantize_mx(y_codes[:, cols].bitcast(E4M3), y_plane[:, cols], y_rounded[:])
-            for lo, hi in STORES:
-                if hi == cols.stop:
-                    nc.sync.dma_start(out_words[:, lo:hi], y_codes[:, lo:hi].bitcast(I32))
+        def pack_y(lo, width, y_rounded):
+            cols = slice(lo, lo + width)
+            nc.vector.quantize_mx(y_codes[:, cols].bitcast(E4M3), y_plane[:, cols], y_rounded[:, : PACK * width])
+            for start, stop in STORES:
+                if stop == cols.stop:
+                    nc.sync.dma_start(out_words[:, start:stop], y_codes[:, start:stop].bitcast(I32))
 
         pairs = len(units) // 2
-        rounded, decoded = {}, {}
-        for pair in range(pairs + 2):
-            if pair < pairs:
-                first, second = 2 * pair, 2 * pair + 1
-                rounded[pair] = ring.tile([P, 2 * PACK * BLOCK], BF16, name="h_rounded", align_bytes=64)
-                scaled_first = style(*units[first])
-                if first in parked:
-                    shift(first, scaled_first, rounded[pair][:, : PACK * BLOCK])
-                scaled_second = style(*units[second])
-                if first not in parked:
-                    shift(first, scaled_first, rounded[pair][:, : PACK * BLOCK])
-                shift(second, scaled_second, rounded[pair][:, PACK * BLOCK :])
-            if 0 <= pair - 1 < pairs:
-                g, jb = units[2 * (pair - 1)]
-                h_q[g, jb // 2] = quantise("h_%d_%d" % (g, jb), rounded[pair - 1], 2 * BLOCK, 2 if pair == pairs else 1)
-            if pair in (2, 3):
-                w1_q[pair - 2, 1] = quantise("w1_%d_1" % (pair - 2), round_weight(w1_raw[pair - 2, 1]), PASS)
-            if pair in (4, 5):
-                w3_q.append(quantise("w3_%d" % (pair - 4), round_weight(w3_raw[pair - 4]), N))
-            for jb in sorted(decoded):
-                pack_y(jb, decoded[jb])
-            decoded = {}
-            if pair - 1 >= pairs // 2:
-                first = 2 * (pair - 1) - BLOCKS
-                for jb in (first, first + 1):
-                    if jb < BLOCKS:
-                        decoded[jb] = decode(jb)
+        scaled, rounded, decoded = {}, {}, []
+        for step in range(pairs + 3):
+            if step < pairs:
+                g, jb = units[2 * step]
+                scaled[step] = ring.tile([P, PACK, PAIR], F32, name="scaled", align_bytes=64)
+                rounded[step] = ring.tile([P, PACK * PAIR], BF16, name="h_rounded", align_bytes=64)
+                scale_rows(g, jb * BLOCK, 0, scaled[step])
+            for args in decoded:
+                pack_y(*args)
+            decoded = []
+            done = step - 2
+            if 0 <= done < pairs:
+                done_g, done_jb = units[2 * done]
+                last = done == pairs - 1
+                h_q[done_g, done_jb // 2] = quantise("h_%d" % done, rounded[done], PAIR, 2 if last else 1)
+            if step in (2, 3):
+                w1_q[step - 2, 1] = quantise("w1_%d_1" % (step - 2), round_weight(w1_raw[step - 2, 1]), PASS)
+            if step in (4, 5):
+                w3_q.append(quantise("w3_%d" % (step - 4), round_weight(w3_raw[step - 4]), N))
+            if 0 <= done < pairs and done_g == 1:
+                width = BLOCK if last else PAIR
+                decoded = [decode(lo, width) for lo in range(done_jb * BLOCK, done_jb * BLOCK + PAIR, width)]
+            if step < pairs:
+                scale_rows(g, jb * BLOCK, 1, scaled[step])
+                if 2 * step in parked:
+                    shift(2 * step, scaled[step], rounded[step])
+            if 0 <= step - 1 < pairs:
+                for u in (2 * step - 2, 2 * step - 1):
+                    if u not in parked:
+                        shift(u, scaled[step - 1], rounded[step - 1])
 
         for q in range(4):
             nc.sync.dma_start(out_2[0, 4 * q : 4 * q + 4, :].bitcast(I32), y_plane[32 * q : 32 * q + 4, :].bitcast(I32))

@@ -18,15 +18,21 @@ MULT = mybir.AluOpType.mult
 IDENTITY = mybir.ActivationFunctionType.Identity
 
 P = 128
-PACK = 4
-PASS = P * PACK
-BLOCK = 128
-BLOCKS = S // BLOCK
-HALF = S // 2
+SLOTS = 4
+PASS = P * SLOTS
+BANK = 512
+BLOCK = BANK // SLOTS
 PAIR = 2 * BLOCK
-X_PIECES = [[(0, 512), (512, 1024)], [(0, 512), (512, 1024)]]
-STORES = [(0, 512), (512, 768), (768, 1024)]
-SHARED = []
+PAIRS = S // PAIR
+HALF = S // 2
+TAB_FIRST_ROW = 4
+
+X_PIECES = [[(0, 256), (256, 512), (512, 1024)], [(0, 512), (512, 1024)]]
+Y_STORES = [(0, 256), (256, 512), (512, 768), (768, 896), (896, 1024)]
+CODE_STORES = [(0, 512), (512, 768), (768, 1024)]
+ROUNDED_ON_VECTOR = (512, 896)
+W1_STEPS = (2, 3)
+W3_STEPS = (4, 5)
 
 
 def tile_list_style_modulated_decoder_kernel(
@@ -43,19 +49,16 @@ def tile_list_style_modulated_decoder_kernel(
         def held(name, shape, dtype):
             return keep.tile(shape, dtype, name=name, align_bytes=64)
 
-        list1 = held("list1", [P, S // 16], U16)
-        list2 = held("list2", [P, S // 16], U16)
-        nc.sync.dma_start(list2[:], offs2)
-        nc.sync.dma_start(list1[:], offs)
-
         w2_plane_raw = held("w2_plane_raw", [P, H], U8)
         tab2_plane = held("tab2_plane", [P, T2], U8)
         tab_plane = held("tab_plane", [P, T], U8)
         for plane in (tab_plane, w2_plane_raw, tab2_plane):
             nc.vector.memset(plane[:].bitcast(I32), 0)
+
         for q in range(4):
+            first = 32 * q + TAB_FIRST_ROW
             nc.gpsimd.dma_start(
-                tab_plane[32 * q + 4 : 32 * q + 12, :].bitcast(I32), tab_scales[:, 4 * q : 4 * q + 4, :].bitcast(I32)
+                tab_plane[first : first + 8, :].bitcast(I32), tab_scales[:, 4 * q : 4 * q + 4, :].bitcast(I32)
             )
 
         def load_plane(plane, scales):
@@ -68,8 +71,8 @@ def tile_list_style_modulated_decoder_kernel(
             return tile
 
         def load_rows(name, rows):
-            tile = held(name, [P, PACK, rows.shape[1]], F32)
-            nc.sync.dma_start(tile[:], rows.rearrange("(p t) c -> p t c", t=PACK))
+            tile = held(name, [P, SLOTS, rows.shape[1]], F32)
+            nc.sync.dma_start(tile[:], rows.rearrange("(p t) c -> p t c", t=SLOTS))
             return tile
 
         def load_w1(a, g):
@@ -82,6 +85,10 @@ def tile_list_style_modulated_decoder_kernel(
         w2_raw = held("w2_raw", [P, 2 * H], U8)
         nc.sync.dma_start(w2_raw[:].bitcast(I32), w2_words[0].bitcast(I32))
         tab2 = load_words("tab2", tab2_words[0], T2)
+        list2 = held("list2", [P, S // 16], U16)
+        nc.sync.dma_start(list2[:], offs2)
+        list1 = held("list1", [P, S // 16], U16)
+        nc.sync.dma_start(list1[:], offs)
         load_plane(w2_plane_raw, w2_scales)
         w1_raw = {}
         x_sb = {}
@@ -90,10 +97,10 @@ def tile_list_style_modulated_decoder_kernel(
         tab = [load_words("tab_0", tab_words[0], T)]
         w1_raw[1, 0] = load_w1(1, 0)
         tab.append(load_words("tab_1", tab_words[1], T))
-        bias = held("bias", [P, PACK], F32)
-        nc.sync.dma_start(bias[:], b3.rearrange("(p t) -> p t", t=PACK))
         for piece in X_PIECES[0]:
             x_sb[0, piece] = load_x(0, piece)
+        bias = held("bias", [P, SLOTS], F32)
+        nc.sync.dma_start(bias[:], b3.rearrange("(p t) -> p t", t=SLOTS))
         w1_raw[0, 1] = load_w1(0, 1)
         w1_raw[1, 1] = load_w1(1, 1)
         w3_raw = []
@@ -101,16 +108,17 @@ def tile_list_style_modulated_decoder_kernel(
             w3_raw.append(load_rows("w3_raw_%d" % g, w3[g * PASS : (g + 1) * PASS, :]))
             x_sb[1, X_PIECES[1][g]] = load_x(1, X_PIECES[1][g])
 
-        def x_block(g, rows, lo, width):
-            piece = X_PIECES[g][lo // HALF]
-            return x_sb[g, piece][:, rows, lo - piece[0] : lo - piece[0] + width]
+        def x_columns(g, slots, lo):
+            piece = [(start, stop) for start, stop in X_PIECES[g] if start <= lo < stop][0]
+            return x_sb[g, piece][:, slots, lo - piece[0] : lo - piece[0] + PAIR]
 
         def gather(name, window, offsets, dtype, parts):
             width = S // parts
             tiles = []
-            for h in range(parts):
-                picked = held("%s_%d" % (name, h), [P, width], dtype)
-                nc.vector.tensor_copy(picked[:], window[:].indirect(offsets[:, h * width // 16 : (h + 1) * width // 16]))
+            for part in range(parts):
+                picked = held("%s_%d" % (name, part), [P, width], dtype)
+                entries = offsets[:, part * width // 16 : (part + 1) * width // 16]
+                nc.vector.tensor_copy(picked[:], window[:].indirect(entries))
                 tiles.append(picked)
             return tiles
 
@@ -119,9 +127,9 @@ def tile_list_style_modulated_decoder_kernel(
             return tiles[lo // width][first_row:P, lo % width : lo % width + count]
 
         def round_weight(raw):
-            dealt = ring.tile([P, PACK * PASS], BF16, name="dealt", align_bytes=64, bufs=4)
+            dealt = ring.tile([P, SLOTS * PASS], BF16, name="dealt", align_bytes=64, bufs=4)
             nc.scalar.copy(
-                dealt[:].rearrange("p (u e m j) -> p u m j e", u=2, e=2, j=PACK),
+                dealt[:].rearrange("p (u e m j) -> p u m j e", u=2, e=2, j=SLOTS),
                 raw[:].rearrange("p j (m u e) -> p u m j e", u=2, e=2),
             )
             return dealt
@@ -129,23 +137,24 @@ def tile_list_style_modulated_decoder_kernel(
         def quantise(name, rounded, width, calls=1):
             codes = held(name + "_codes", [P, width], U32)
             plane = held(name + "_plane", [P, width], U8)
-            step = width // calls
-            for lo in range(0, width, step):
+            each = width // calls
+            for lo in range(0, width, each):
                 nc.vector.quantize_mx(
-                    codes[:, lo : lo + step].bitcast(E4M3), plane[:, lo : lo + step], rounded[:, PACK * lo : PACK * (lo + step)]
+                    codes[:, lo : lo + each].bitcast(E4M3), plane[:, lo : lo + each],
+                    rounded[:, SLOTS * lo : SLOTS * (lo + each)],
                 )
             return codes, plane
 
         w2_dealt = held("w2_dealt", [P, 2 * H], U8)
         nc.vector.tensor_copy(
-            w2_dealt[:].bitcast(U16).rearrange("p (g t m) -> p g t m", g=2, t=PACK),
-            w2_raw[:].bitcast(U16).rearrange("p (g m t) -> p g t m", g=2, t=PACK),
+            w2_dealt[:].bitcast(U16).rearrange("p (g t m) -> p g t m", g=2, t=SLOTS),
+            w2_raw[:].bitcast(U16).rearrange("p (g m t) -> p g t m", g=2, t=SLOTS),
         )
         v2_words = gather("v2_words", tab2, list2, U32, 1)
         w2_plane = held("w2_plane", [P, H], U8)
         nc.vector.tensor_copy(
-            w2_plane[:].rearrange("p (g t m) -> p g t m", g=2, t=PACK),
-            w2_plane_raw[:].rearrange("p (g m t) -> p g t m", g=2, t=PACK),
+            w2_plane[:].rearrange("p (g t m) -> p g t m", g=2, t=SLOTS),
+            w2_plane_raw[:].rearrange("p (g m t) -> p g t m", g=2, t=SLOTS),
         )
         w1_q = {}
         w1_q[0, 0] = quantise("w1_0_0", round_weight(w1_raw[0, 0]), PASS)
@@ -155,134 +164,139 @@ def tile_list_style_modulated_decoder_kernel(
         w1_q[1, 0] = quantise("w1_1_0", round_weight(w1_raw[1, 0]), PASS)
         v_words.append(gather("v_words_1", tab[1], list1, U32, 2))
 
-        def scale_rows(g, lo, u, scaled):
+        def scale_slots(g, lo, u, scaled):
             a_bank = psum.tile([P, 2, PAIR], F32, name="a_bank")
             for a in range(2):
                 codes, plane = w1_q[a, g]
                 for e in range(2):
-                    cols = slice((2 * u + e) * P, (2 * u + e + 1) * P)
+                    places = slice((2 * u + e) * P, (2 * u + e + 1) * P)
                     nc.tensor.matmul_mx(
                         a_bank[:, e, :],
-                        lhsT=codes[:, cols].bitcast(E4M3), lhsT_scale=plane[:, cols],
-                        rhs=columns(v_words[a], lo, PAIR).bitcast(E4M3), rhs_scale=columns(v_plane, lo, PAIR, 4 + 4 * a),
-                        start=(a == 0 and e == 0), stop=(a == 1 and e == 1),
+                        lhsT=codes[:, places].bitcast(E4M3),
+                        lhsT_scale=plane[:, places],
+                        rhs=columns(v_words[a], lo, PAIR).bitcast(E4M3),
+                        rhs_scale=columns(v_plane, lo, PAIR, TAB_FIRST_ROW + 4 * a),
+                        start=(a == 0 and e == 0),
+                        stop=(a == 1 and e == 1),
                     )
-            rows = slice(2 * u, 2 * u + 2)
-            nc.vector.scalar_tensor_tensor(scaled[:, rows, :], a_bank[:], 1.0, x_block(g, rows, lo, PAIR), ADD, MULT)
+            slots = slice(2 * u, 2 * u + 2)
+            nc.vector.scalar_tensor_tensor(scaled[:, slots, :], a_bank[:], 1.0, x_columns(g, slots, lo), ADD, MULT)
 
-        def shift_product(g, jb):
-            b_bank = psum.tile([P, PACK, BLOCK], F32, name="b_bank")
-            for t in range(PACK):
-                lo = g * PASS + t * P
-                nc.tensor.matmul_mx(
-                    b_bank[:, t, :],
-                    lhsT=w2_dealt[:, 2 * lo : 2 * (lo + P)].bitcast(E2M1), lhsT_scale=w2_plane[:, lo : lo + P],
-                    rhs=columns(v2_words, jb * BLOCK, BLOCK).bitcast(E4M3), rhs_scale=columns(v2_plane, jb * BLOCK, BLOCK),
-                    start=True, stop=True,
-                )
-            return b_bank
-
-        units = [(g, jb) for g in range(2) for jb in range(BLOCKS)]
-        parked = {}
-        for u in SHARED:
-            parked[u] = held("parked_%d" % u, [P, BLOCK, PACK], F32)
-            nc.scalar.copy(parked[u][:], shift_product(*units[u])[:].rearrange("p t j -> p j t"))
-
-        def shift(u, scaled, h_rounded):
-            at = u % 2 * BLOCK
-            scaled_block = scaled[:, :, at : at + BLOCK]
-            h_block = h_rounded[:, PACK * at : PACK * (at + BLOCK)]
-            if u in parked:
-                nc.gpsimd.tensor_tensor(
-                    h_block.rearrange("p (j t) -> p j t", t=PACK), parked[u][:],
-                    scaled_block.rearrange("p t j -> p j t"), ADD,
-                )
-            else:
+        def add_shift(g, lo, scaled):
+            h_rounded = ring.tile([P, SLOTS * PAIR], BF16, name="h_rounded", align_bytes=64)
+            for at in range(0, PAIR, BLOCK):
+                b_bank = psum.tile([P, SLOTS, BLOCK], F32, name="b_bank")
+                for t in range(SLOTS):
+                    place = g * PASS + t * P
+                    nc.tensor.matmul_mx(
+                        b_bank[:, t, :],
+                        lhsT=w2_dealt[:, 2 * place : 2 * (place + P)].bitcast(E2M1),
+                        lhsT_scale=w2_plane[:, place : place + P],
+                        rhs=columns(v2_words, lo + at, BLOCK).bitcast(E4M3),
+                        rhs_scale=columns(v2_plane, lo + at, BLOCK),
+                        start=True,
+                        stop=True,
+                    )
                 nc.vector.tensor_tensor(
-                    h_block.rearrange("p (c i t) -> p c t i", i=2, t=PACK),
-                    shift_product(*units[u])[:].rearrange("p t (c i) -> p c t i", i=2),
-                    scaled_block.rearrange("p t (c i) -> p c t i", i=2),
+                    h_rounded[:, SLOTS * at : SLOTS * (at + BLOCK)].rearrange("p (c i t) -> p c t i", i=2, t=SLOTS),
+                    b_bank[:].rearrange("p t (c i) -> p c t i", i=2),
+                    scaled[:, :, at : at + BLOCK].rearrange("p t (c i) -> p c t i", i=2),
                     ADD,
                 )
+            return h_rounded
 
-        y_plane = held("y_plane", [P, S], U8)
-        y_sb = [held("w1_raw_%d_0" % s, [P, PACK, HALF], F32) for s in range(2)]
+        y_sb = [held("w1_raw_%d_0" % half, [P, SLOTS, HALF], F32) for half in range(2)]
         y_codes = held("y_codes", [P, S], U32)
-        out_rows = out_0.rearrange("(p t) j -> p t j", t=PACK)
+        y_plane = held("y_plane", [P, S], U8)
+        out_rows = out_0.rearrange("(p t) j -> p t j", t=SLOTS)
         out_words = out_1[0].rearrange("p m t -> p (m t)").bitcast(I32)
         h_q = {}
         w3_q = []
 
         def decode(lo, width):
             half, at = divmod(lo, HALF)
-            y_block = y_sb[half][:, :, at : at + width]
-            slots = PASS // width
-            for first in range(0, PACK, slots):
-                y_bank = psum_y.tile([P, slots, width], F32, name="y_bank")
-                for e in range(slots):
-                    cols = slice((first + e) * P, (first + e + 1) * P)
+            y_part = y_sb[half][:, :, at : at + width]
+            per_bank = BANK // width
+            in_pair = slice(lo % PAIR, lo % PAIR + width)
+            for first in range(0, SLOTS, per_bank):
+                if width == BLOCK:
+                    y_bank = psum.tile([P, per_bank, width], F32, name="a_bank")
+                else:
+                    y_bank = psum_y.tile([P, per_bank, width], F32, name="y_bank")
+                for e in range(per_bank):
+                    places = slice((first + e) * P, (first + e + 1) * P)
                     for g in range(2):
                         codes, plane = w3_q[g]
-                        h_codes, h_plane = h_q[g, lo // PAIR]
-                        h_cols = slice(lo % PAIR, lo % PAIR + width)
+                        h_codes, h_plane = h_q[g, lo - lo % PAIR]
                         nc.tensor.matmul_mx(
                             y_bank[:, e, :],
-                            lhsT=codes[:, cols].bitcast(E4M3), lhsT_scale=plane[:, cols],
-                            rhs=h_codes[:, h_cols].bitcast(E4M3), rhs_scale=h_plane[:, h_cols],
-                            start=(g == 0), stop=(g == 1),
+                            lhsT=codes[:, places].bitcast(E4M3),
+                            lhsT_scale=plane[:, places],
+                            rhs=h_codes[:, in_pair].bitcast(E4M3),
+                            rhs_scale=h_plane[:, in_pair],
+                            start=(g == 0),
+                            stop=(g == 1),
                         )
-                for e in range(slots):
-                    t = first + e
-                    nc.scalar.activation(y_block[:, t, :], y_bank[:, e, :], IDENTITY, bias=bias[:, t : t + 1])
-            for start, stop in STORES:
+                if lo + width == S:
+                    spread = bias[:].unsqueeze(2).to_broadcast([P, SLOTS, BLOCK])
+                    nc.vector.tensor_tensor(y_part, y_bank[:], spread, ADD)
+                else:
+                    for e in range(per_bank):
+                        t = first + e
+                        nc.scalar.activation(y_part[:, t, :], y_bank[:, e, :], IDENTITY, bias=bias[:, t : t + 1])
+            for start, stop in Y_STORES:
                 if stop == lo + width:
-                    nc.sync.dma_start(out_rows[:, :, start:stop], y_sb[half][:, :, start - half * HALF : stop - half * HALF])
-            y_rounded = ring.tile([P, PACK * PAIR], BF16, name="y_rounded", align_bytes=64)
-            copy = nc.vector.tensor_copy if lo + width == S else nc.scalar.copy
+                    nc.sync.dma_start(
+                        out_rows[:, :, start:stop], y_sb[half][:, :, start - half * HALF : stop - half * HALF]
+                    )
+            y_rounded = ring.tile([P, SLOTS * PAIR], BF16, name="y_rounded", align_bytes=64)
+            copy = nc.vector.tensor_copy if lo in ROUNDED_ON_VECTOR else nc.scalar.copy
             copy(
-                y_rounded[:, : PACK * width].rearrange("p (c i t) -> p c t i", i=2, t=PACK),
-                y_block.rearrange("p t (c i) -> p c t i", i=2),
+                y_rounded[:, : SLOTS * width].rearrange("p (c i t) -> p c t i", i=2, t=SLOTS),
+                y_part.rearrange("p t (c i) -> p c t i", i=2),
             )
             return lo, width, y_rounded
 
         def pack_y(lo, width, y_rounded):
             cols = slice(lo, lo + width)
-            nc.vector.quantize_mx(y_codes[:, cols].bitcast(E4M3), y_plane[:, cols], y_rounded[:, : PACK * width])
-            for start, stop in STORES:
+            nc.vector.quantize_mx(y_codes[:, cols].bitcast(E4M3), y_plane[:, cols], y_rounded[:, : SLOTS * width])
+            for start, stop in CODE_STORES:
                 if stop == cols.stop:
                     nc.sync.dma_start(out_words[:, start:stop], y_codes[:, start:stop].bitcast(I32))
 
-        pairs = len(units) // 2
-        scaled, rounded, decoded = {}, {}, []
-        for step in range(pairs + 3):
-            if step < pairs:
-                g, jb = units[2 * step]
-                scaled[step] = ring.tile([P, PACK, PAIR], F32, name="scaled", align_bytes=64)
-                rounded[step] = ring.tile([P, PACK * PAIR], BF16, name="h_rounded", align_bytes=64)
-                scale_rows(g, jb * BLOCK, 0, scaled[step])
-            for args in decoded:
-                pack_y(*args)
+        steps = [(g, lo) for g in range(2) for lo in range(0, S, PAIR)]
+        scaled = {}
+        waiting = []
+        decoded = []
+        for step in range(len(steps) + 2):
+            own = step < len(steps)
+            before = 1 <= step <= len(steps)
+            if own:
+                scaled[step] = ring.tile([P, SLOTS, PAIR], F32, name="scaled", align_bytes=64)
+                scale_slots(*steps[step], 0, scaled[step])
+            if before:
+                h_rounded = add_shift(*steps[step - 1], scaled[step - 1])
+            if step in W1_STEPS:
+                a = W1_STEPS.index(step)
+                w1_q[a, 1] = quantise("w1_%d_1" % a, round_weight(w1_raw[a, 1]), PASS)
+            if step in W3_STEPS:
+                w3_q.append(quantise("w3_%d" % step, round_weight(w3_raw[W3_STEPS.index(step)]), N))
+            if own:
+                scale_slots(*steps[step], 1, scaled[step])
+            if before:
+                g, lo = steps[step - 1]
+                width = PAIR if own else BLOCK
+                h_q[g, lo] = quantise("h_%d" % step, h_rounded, PAIR, PAIR // width)
+                if g == 1:
+                    waiting.extend((first, width) for first in range(lo, lo + PAIR, width))
+            for stretch in decoded:
+                pack_y(*stretch)
             decoded = []
-            done = step - 2
-            if 0 <= done < pairs:
-                done_g, done_jb = units[2 * done]
-                last = done == pairs - 1
-                h_q[done_g, done_jb // 2] = quantise("h_%d" % done, rounded[done], PAIR, 2 if last else 1)
-            if step in (2, 3):
-                w1_q[step - 2, 1] = quantise("w1_%d_1" % (step - 2), round_weight(w1_raw[step - 2, 1]), PASS)
-            if step in (4, 5):
-                w3_q.append(quantise("w3_%d" % (step - 4), round_weight(w3_raw[step - 4]), N))
-            if 0 <= done < pairs and done_g == 1:
-                width = BLOCK if last else PAIR
-                decoded = [decode(lo, width) for lo in range(done_jb * BLOCK, done_jb * BLOCK + PAIR, width)]
-            if step < pairs:
-                scale_rows(g, jb * BLOCK, 1, scaled[step])
-                if 2 * step in parked:
-                    shift(2 * step, scaled[step], rounded[step])
-            if 0 <= step - 1 < pairs:
-                for u in (2 * step - 2, 2 * step - 1):
-                    if u not in parked:
-                        shift(u, scaled[step - 1], rounded[step - 1])
+            if len(w3_q) == 2:
+                decoded = [decode(first, width) for first, width in waiting]
+                waiting = []
 
         for q in range(4):
-            nc.sync.dma_start(out_2[0, 4 * q : 4 * q + 4, :].bitcast(I32), y_plane[32 * q : 32 * q + 4, :].bitcast(I32))
+            nc.scalar.dma_start(
+                out_2[0, 4 * q : 4 * q + 4, :].bitcast(I32), y_plane[32 * q : 32 * q + 4, :].bitcast(I32)
+            )

@@ -27,12 +27,11 @@ PAIRS = S // PAIR
 HALF = S // 2
 TAB_FIRST_ROW = 4
 
-X_PIECES = [[(0, 256), (256, 512), (512, 1024)], [(0, 512), (512, 1024)]]
+STEPS = [(0, 0), (0, 256), (0, 512), (1, 0), (1, 256), (1, 512), (0, 768), (1, 768)]
 Y_STORES = [(0, 256), (256, 512), (512, 768), (768, 896), (896, 1024)]
-CODE_STORES = [(0, 512), (512, 768), (768, 1024)]
 ROUNDED_ON_VECTOR = (512, 896)
-W1_STEPS = (2, 3)
-W3_STEPS = (4, 5)
+GPSIMD_STEPS = (4, 6)
+H_BUFFERS = ["h_0", "h_1", "h_0", "h_1", "rounded_1", "h_0", "h_0"]
 
 
 def tile_list_style_modulated_decoder_kernel(
@@ -52,7 +51,7 @@ def tile_list_style_modulated_decoder_kernel(
         w2_plane_raw = held("w2_plane_raw", [P, H], U8)
         tab2_plane = held("tab2_plane", [P, T2], U8)
         tab_plane = held("tab_plane", [P, T], U8)
-        for plane in (tab_plane, w2_plane_raw, tab2_plane):
+        for plane in (tab2_plane, tab_plane, w2_plane_raw):
             nc.vector.memset(plane[:].bitcast(I32), 0)
 
         for q in range(4):
@@ -70,47 +69,49 @@ def tile_list_style_modulated_decoder_kernel(
             nc.sync.dma_start(tile[:].bitcast(I32), words.rearrange("p n t -> p (n t)").bitcast(I32))
             return tile
 
-        def load_rows(name, rows):
+        def load_rows(name, rows, parts=1):
             tile = held(name, [P, SLOTS, rows.shape[1]], F32)
-            nc.sync.dma_start(tile[:], rows.rearrange("(p t) c -> p t c", t=SLOTS))
+            by_slot = rows.rearrange("(p t) c -> p t c", t=SLOTS)
+            each = SLOTS // parts
+            for t in range(0, SLOTS, each):
+                nc.sync.dma_start(tile[:, t : t + each, :], by_slot[:, t : t + each, :])
             return tile
 
         def load_w1(a, g):
             return load_rows("w1_raw_%d_%d" % (a, g), w1[a * PASS : (a + 1) * PASS, g * PASS : (g + 1) * PASS])
 
-        def load_x(g, piece):
-            lo, hi = piece
-            return load_rows("x_%d_%d" % (g, lo), x[g * PASS : (g + 1) * PASS, lo:hi])
+        def load_x(steps, parts=1):
+            g, lo = STEPS[steps[0]]
+            tile = load_rows("x_%d" % steps[0], x[g * PASS : (g + 1) * PASS, lo : lo + PAIR * len(steps)], parts)
+            for k, step in enumerate(steps):
+                x_sb[step] = tile[:, :, k * PAIR : (k + 1) * PAIR]
 
         w2_raw = held("w2_raw", [P, 2 * H], U8)
         nc.sync.dma_start(w2_raw[:].bitcast(I32), w2_words[0].bitcast(I32))
-        tab2 = load_words("tab2", tab2_words[0], T2)
         list2 = held("list2", [P, S // 16], U16)
         nc.sync.dma_start(list2[:], offs2)
+        tab2 = load_words("tab2", tab2_words[0], T2)
+        load_plane(tab2_plane, tab2_scales)
+        tab = [load_words("tab_0", tab_words[0], T)]
         list1 = held("list1", [P, S // 16], U16)
         nc.sync.dma_start(list1[:], offs)
-        load_plane(w2_plane_raw, w2_scales)
         w1_raw = {}
         x_sb = {}
         w1_raw[0, 0] = load_w1(0, 0)
-        load_plane(tab2_plane, tab2_scales)
-        tab = [load_words("tab_0", tab_words[0], T)]
+        load_plane(w2_plane_raw, w2_scales)
         w1_raw[1, 0] = load_w1(1, 0)
         tab.append(load_words("tab_1", tab_words[1], T))
-        for piece in X_PIECES[0]:
-            x_sb[0, piece] = load_x(0, piece)
-        bias = held("bias", [P, SLOTS], F32)
-        nc.sync.dma_start(bias[:], b3.rearrange("(p t) -> p t", t=SLOTS))
+        load_x([0, 1], parts=2)
         w1_raw[0, 1] = load_w1(0, 1)
         w1_raw[1, 1] = load_w1(1, 1)
-        w3_raw = []
-        for g in range(2):
-            w3_raw.append(load_rows("w3_raw_%d" % g, w3[g * PASS : (g + 1) * PASS, :]))
-            x_sb[1, X_PIECES[1][g]] = load_x(1, X_PIECES[1][g])
-
-        def x_columns(g, slots, lo):
-            piece = [(start, stop) for start, stop in X_PIECES[g] if start <= lo < stop][0]
-            return x_sb[g, piece][:, slots, lo - piece[0] : lo - piece[0] + PAIR]
+        load_x([2])
+        load_x([3, 4])
+        w3_raw = [load_rows("w3_raw_%d" % g, w3[g * PASS : (g + 1) * PASS, :]) for g in range(2)]
+        load_x([5])
+        bias = held("bias", [P, SLOTS], F32)
+        nc.sync.dma_start(bias[:], b3.rearrange("(p t) -> p t", t=SLOTS))
+        load_x([6])
+        load_x([7])
 
         def gather(name, window, offsets, dtype, parts):
             width = S // parts
@@ -126,8 +127,8 @@ def tile_list_style_modulated_decoder_kernel(
             width = S // len(tiles)
             return tiles[lo // width][first_row:P, lo % width : lo % width + count]
 
-        def round_weight(raw):
-            dealt = ring.tile([P, SLOTS * PASS], BF16, name="dealt", align_bytes=64, bufs=4)
+        def round_weight(raw, buffer):
+            dealt = held("rounded_%d" % buffer, [P, SLOTS * PASS], BF16)
             nc.scalar.copy(
                 dealt[:].rearrange("p (u e m j) -> p u m j e", u=2, e=2, j=SLOTS),
                 raw[:].rearrange("p j (m u e) -> p u m j e", u=2, e=2),
@@ -151,20 +152,21 @@ def tile_list_style_modulated_decoder_kernel(
             w2_raw[:].bitcast(U16).rearrange("p (g m t) -> p g t m", g=2, t=SLOTS),
         )
         v2_words = gather("v2_words", tab2, list2, U32, 1)
+        v2_plane = gather("v2_plane", tab2_plane, list2, U8, 1)
+        v_words = [gather("v_words_0", tab[0], list1, U32, 1)]
         w2_plane = held("w2_plane", [P, H], U8)
         nc.vector.tensor_copy(
             w2_plane[:].rearrange("p (g t m) -> p g t m", g=2, t=SLOTS),
             w2_plane_raw[:].rearrange("p (g m t) -> p g t m", g=2, t=SLOTS),
         )
-        w1_q = {}
-        w1_q[0, 0] = quantise("w1_0_0", round_weight(w1_raw[0, 0]), PASS)
-        v2_plane = gather("v2_plane", tab2_plane, list2, U8, 1)
-        v_words = [gather("v_words_0", tab[0], list1, U32, 1)]
         v_plane = gather("v_plane", tab_plane, list1, U8, 1)
-        w1_q[1, 0] = quantise("w1_1_0", round_weight(w1_raw[1, 0]), PASS)
+        w1_q = {}
+        w1_q[0, 0] = quantise("w1_0_0", round_weight(w1_raw[0, 0], 0), PASS)
+        w1_q[1, 0] = quantise("w1_1_0", round_weight(w1_raw[1, 0], 1), PASS)
         v_words.append(gather("v_words_1", tab[1], list1, U32, 2))
 
-        def scale_slots(g, lo, u, scaled):
+        def scale_slots(step, u, scaled):
+            g, lo = STEPS[step]
             a_bank = psum.tile([P, 2, PAIR], F32, name="a_bank")
             for a in range(2):
                 codes, plane = w1_q[a, g]
@@ -179,34 +181,44 @@ def tile_list_style_modulated_decoder_kernel(
                         start=(a == 0 and e == 0),
                         stop=(a == 1 and e == 1),
                     )
-            slots = slice(2 * u, 2 * u + 2)
-            nc.vector.scalar_tensor_tensor(scaled[:, slots, :], a_bank[:], 1.0, x_columns(g, slots, lo), ADD, MULT)
+            x_part = x_sb[step][:, 2 * u : 2 * u + 2, :].rearrange("p e c -> p c e")
+            nc.vector.scalar_tensor_tensor(scaled[:, u], a_bank[:].rearrange("p e c -> p c e"), 1.0, x_part, ADD, MULT)
 
-        def add_shift(g, lo, scaled):
-            h_rounded = ring.tile([P, SLOTS * PAIR], BF16, name="h_rounded", align_bytes=64)
-            for at in range(0, PAIR, BLOCK):
-                b_bank = psum.tile([P, SLOTS, BLOCK], F32, name="b_bank")
-                for t in range(SLOTS):
-                    place = g * PASS + t * P
-                    nc.tensor.matmul_mx(
-                        b_bank[:, t, :],
-                        lhsT=w2_dealt[:, 2 * place : 2 * (place + P)].bitcast(E2M1),
-                        lhsT_scale=w2_plane[:, place : place + P],
-                        rhs=columns(v2_words, lo + at, BLOCK).bitcast(E4M3),
-                        rhs_scale=columns(v2_plane, lo + at, BLOCK),
-                        start=True,
-                        stop=True,
-                    )
-                nc.vector.tensor_tensor(
-                    h_rounded[:, SLOTS * at : SLOTS * (at + BLOCK)].rearrange("p (c i t) -> p c t i", i=2, t=SLOTS),
-                    b_bank[:].rearrange("p t (c i) -> p c t i", i=2),
-                    scaled[:, :, at : at + BLOCK].rearrange("p t (c i) -> p c t i", i=2),
-                    ADD,
+        def shift_block(g, lo):
+            b_bank = psum.tile([P, SLOTS, BLOCK], F32, name="b_bank")
+            for t in range(SLOTS):
+                place = g * PASS + t * P
+                nc.tensor.matmul_mx(
+                    b_bank[:, t, :],
+                    lhsT=w2_dealt[:, 2 * place : 2 * (place + P)].bitcast(E2M1),
+                    lhsT_scale=w2_plane[:, place : place + P],
+                    rhs=columns(v2_words, lo, BLOCK).bitcast(E4M3),
+                    rhs_scale=columns(v2_plane, lo, BLOCK),
+                    start=True,
+                    stop=True,
                 )
-            return h_rounded
+            return b_bank[:].rearrange("p t c -> p c t")
 
-        y_sb = [held("w1_raw_%d_0" % half, [P, SLOTS, HALF], F32) for half in range(2)]
-        y_codes = held("y_codes", [P, S], U32)
+        parked_tile = held("w1_raw_1_0", [P, len(GPSIMD_STEPS), 2, BLOCK, 2], F32)
+        parked = {}
+        for k, step in enumerate(GPSIMD_STEPS):
+            parked[step] = parked_tile[:, k]
+            nc.scalar.copy(parked[step], shift_block(*STEPS[step]).rearrange("p c (u e) -> p u c e", e=2))
+
+        def add_shift(step, scaled, buffer, start, stop):
+            g, lo = STEPS[step]
+            h_rounded = held(buffer, [P, stop - start, 2, 2], BF16)
+            for at in range(start, stop, BLOCK):
+                h_block = h_rounded[:, at - start : at - start + BLOCK]
+                scaled_block = scaled[:, :, at : at + BLOCK, :]
+                if at == 0 and step in parked:
+                    nc.gpsimd.tensor_tensor(h_block.rearrange("p c u e -> p u c e"), parked[step], scaled_block, ADD)
+                else:
+                    shift = shift_block(g, lo + at).rearrange("p c (u e) -> p c u e", e=2)
+                    nc.vector.tensor_tensor(h_block, shift, scaled_block.rearrange("p u c e -> p c u e"), ADD)
+            return h_rounded[:].rearrange("p c u e -> p (c u e)")
+
+        y_sb = [held("w1_raw_0_%d" % half, [P, SLOTS, HALF], F32) for half in range(2)]
         y_plane = held("y_plane", [P, S], U8)
         out_rows = out_0.rearrange("(p t) j -> p t j", t=SLOTS)
         out_words = out_1[0].rearrange("p m t -> p (m t)").bitcast(I32)
@@ -216,30 +228,32 @@ def tile_list_style_modulated_decoder_kernel(
         def decode(lo, width):
             half, at = divmod(lo, HALF)
             y_part = y_sb[half][:, :, at : at + width]
-            per_bank = BANK // width
-            in_pair = slice(lo % PAIR, lo % PAIR + width)
+            very_last = lo + width == S
+            per_bank = 2 if very_last else BANK // width
             for first in range(0, SLOTS, per_bank):
                 if width == BLOCK:
                     y_bank = psum.tile([P, per_bank, width], F32, name="a_bank")
                 else:
                     y_bank = psum_y.tile([P, per_bank, width], F32, name="y_bank")
-                for e in range(per_bank):
-                    places = slice((first + e) * P, (first + e + 1) * P)
-                    for g in range(2):
-                        codes, plane = w3_q[g]
-                        h_codes, h_plane = h_q[g, lo - lo % PAIR]
+                for g in range(2):
+                    codes, plane = w3_q[g]
+                    h_codes, h_plane, h_first = h_q[g, lo]
+                    in_tile = slice(lo - h_first, lo - h_first + width)
+                    for e in range(per_bank):
+                        places = slice((first + e) * P, (first + e + 1) * P)
                         nc.tensor.matmul_mx(
                             y_bank[:, e, :],
                             lhsT=codes[:, places].bitcast(E4M3),
                             lhsT_scale=plane[:, places],
-                            rhs=h_codes[:, in_pair].bitcast(E4M3),
-                            rhs_scale=h_plane[:, in_pair],
-                            start=(g == 0),
-                            stop=(g == 1),
+                            rhs=h_codes[:, in_tile].bitcast(E4M3),
+                            rhs_scale=h_plane[:, in_tile],
+                            start=(g == 0 and e == 0),
+                            stop=(g == 1 and e == per_bank - 1),
                         )
-                if lo + width == S:
-                    spread = bias[:].unsqueeze(2).to_broadcast([P, SLOTS, BLOCK])
-                    nc.vector.tensor_tensor(y_part, y_bank[:], spread, ADD)
+                slots = slice(first, first + per_bank)
+                if very_last and first > 0:
+                    spread = bias[:, slots].unsqueeze(2).to_broadcast([P, per_bank, width])
+                    nc.vector.tensor_tensor(y_part[:, slots, :], y_bank[:], spread, ADD)
                 else:
                     for e in range(per_bank):
                         t = first + e
@@ -249,7 +263,10 @@ def tile_list_style_modulated_decoder_kernel(
                     nc.sync.dma_start(
                         out_rows[:, :, start:stop], y_sb[half][:, :, start - half * HALF : stop - half * HALF]
                     )
-            y_rounded = ring.tile([P, SLOTS * PAIR], BF16, name="y_rounded", align_bytes=64)
+            return lo, width, y_part
+
+        def round_y(lo, width, y_part):
+            y_rounded = held("y_rounded_%d" % lo, [P, SLOTS * width], BF16)
             copy = nc.vector.tensor_copy if lo in ROUNDED_ON_VECTOR else nc.scalar.copy
             copy(
                 y_rounded[:, : SLOTS * width].rearrange("p (c i t) -> p c t i", i=2, t=SLOTS),
@@ -257,44 +274,60 @@ def tile_list_style_modulated_decoder_kernel(
             )
             return lo, width, y_rounded
 
-        def pack_y(lo, width, y_rounded):
-            cols = slice(lo, lo + width)
-            nc.vector.quantize_mx(y_codes[:, cols].bitcast(E4M3), y_plane[:, cols], y_rounded[:, : SLOTS * width])
-            for start, stop in CODE_STORES:
-                if stop == cols.stop:
-                    nc.sync.dma_start(out_words[:, start:stop], y_codes[:, start:stop].bitcast(I32))
+        def pack_y(buffer, *stretches):
+            start = stretches[0][0]
+            stop = stretches[-1][0] + stretches[-1][1]
+            codes = held(buffer, [P, stop - start], U32)
+            for lo, width, y_rounded in stretches:
+                nc.vector.quantize_mx(
+                    codes[:, lo - start : lo - start + width].bitcast(E4M3), y_plane[:, lo : lo + width], y_rounded[:]
+                )
+            nc.sync.dma_start(out_words[:, start:stop], codes[:].bitcast(I32))
 
-        steps = [(g, lo) for g in range(2) for lo in range(0, S, PAIR)]
+        def pack_h(g, lo, width, h_rounded):
+            codes, plane = quantise("h_%d_%d" % (g, lo), h_rounded, width)
+            for first in range(lo, lo + width, BLOCK):
+                h_q[g, first] = (codes, plane, lo)
+
         scaled = {}
-        waiting = []
+        h_rounded = {}
         decoded = []
-        for step in range(len(steps) + 2):
-            own = step < len(steps)
-            before = 1 <= step <= len(steps)
-            if own:
-                scaled[step] = ring.tile([P, SLOTS, PAIR], F32, name="scaled", align_bytes=64)
-                scale_slots(*steps[step], 0, scaled[step])
-            if before:
-                h_rounded = add_shift(*steps[step - 1], scaled[step - 1])
-            if step in W1_STEPS:
-                a = W1_STEPS.index(step)
-                w1_q[a, 1] = quantise("w1_%d_1" % a, round_weight(w1_raw[a, 1]), PASS)
-            if step in W3_STEPS:
-                w3_q.append(quantise("w3_%d" % step, round_weight(w3_raw[W3_STEPS.index(step)]), N))
-            if own:
-                scale_slots(*steps[step], 1, scaled[step])
-            if before:
-                g, lo = steps[step - 1]
-                width = PAIR if own else BLOCK
-                h_q[g, lo] = quantise("h_%d" % step, h_rounded, PAIR, PAIR // width)
-                if g == 1:
-                    waiting.extend((first, width) for first in range(lo, lo + PAIR, width))
-            for stretch in decoded:
-                pack_y(*stretch)
-            decoded = []
-            if len(w3_q) == 2:
-                decoded = [decode(first, width) for first, width in waiting]
-                waiting = []
+        last = len(STEPS) - 1
+        for step in range(len(STEPS)):
+            if step == 3:
+                w1_q[1, 1] = quantise("w1_1_1", round_weight(w1_raw[1, 1], 3), PASS)
+            scaled[step] = ring.tile([P, 2, PAIR, 2], F32, name="scaled", align_bytes=64)
+            scale_slots(step, 0, scaled[step])
+            if step == 5:
+                w3_q.append(quantise("w3_1", round_weight(w3_raw[1], 1), N))
+                decoded.append(round_y(*decode(STEPS[3][1], PAIR)))
+            if step >= 1:
+                h_rounded[step - 1] = add_shift(step - 1, scaled[step - 1], H_BUFFERS[step - 1], 0, PAIR)
+            scale_slots(step, 1, scaled[step])
+            if step == 2:
+                w1_q[0, 1] = quantise("w1_0_1", round_weight(w1_raw[0, 1], 2), PASS)
+            if step == 4:
+                w3_q.append(quantise("w3_0", round_weight(w3_raw[0], 0), N))
+            for earlier in range(step):
+                if step == earlier + (2 if earlier in parked else 1) and earlier < last - 1:
+                    pack_h(*STEPS[earlier], PAIR, h_rounded[earlier])
+            if step == 6:
+                second_pair = decode(STEPS[4][1], PAIR)
+                third_pair = decode(STEPS[5][1], PAIR)
+                decoded.append(round_y(*second_pair))
+        pack_y("y_codes_0", decoded[0])
+        g, lo = STEPS[last]
+        h_first_block = add_shift(last, scaled[last], "rounded_3", 0, BLOCK)
+        pack_h(*STEPS[last - 1], PAIR, h_rounded[last - 1])
+        pack_h(g, lo, BLOCK, h_first_block)
+        first_block = decode(lo, BLOCK)
+        h_second_block = add_shift(last, scaled[last], "rounded_2", BLOCK, PAIR)
+        pack_y("rounded_3", decoded[1])
+        pack_h(g, lo + BLOCK, BLOCK, h_second_block)
+        decoded.append(round_y(*third_pair))
+        second_block = decode(lo + BLOCK, BLOCK)
+        pack_y("rounded_2", decoded[2])
+        pack_y("y_codes", round_y(*first_block), round_y(*second_block))
 
         for q in range(4):
             nc.scalar.dma_start(

@@ -30,8 +30,9 @@ TAB_FIRST_ROW = 4
 STEPS = [(0, 0), (0, 256), (0, 512), (1, 0), (1, 256), (1, 512), (0, 768), (1, 768)]
 Y_STORES = [(0, 256), (256, 512), (512, 768), (768, 896), (896, 1024)]
 ROUNDED_ON_VECTOR = (512, 896)
-GPSIMD_STEPS = (4, 6)
-H_BUFFERS = ["h_0", "h_1", "h_0", "h_1", "rounded_1", "h_0", "h_0"]
+GPSIMD_STEPS = (5, 6)
+H_BUFFERS = ["h_0", "h_1", "h_0", "h_1", "h_0", "h_0", "h_0"]
+H_CODE_BUFFERS = {4: "rounded_1"}
 
 
 def tile_list_style_modulated_decoder_kernel(
@@ -77,8 +78,13 @@ def tile_list_style_modulated_decoder_kernel(
                 nc.sync.dma_start(tile[:, t : t + each, :], by_slot[:, t : t + each, :])
             return tile
 
-        def load_w1(a, g):
-            return load_rows("w1_raw_%d_%d" % (a, g), w1[a * PASS : (a + 1) * PASS, g * PASS : (g + 1) * PASS])
+        def load_weight(name, rows, pieces=1):
+            width = PASS // pieces
+            return [load_rows("%s_%d" % (name, k), rows[:, k * width : (k + 1) * width]) for k in range(pieces)]
+
+        def load_w1(a, g, pieces=1):
+            rows = w1[a * PASS : (a + 1) * PASS, g * PASS : (g + 1) * PASS]
+            return load_weight("w1_raw_%d_%d" % (a, g), rows, pieces)
 
         def load_x(steps, parts=1):
             g, lo = STEPS[steps[0]]
@@ -106,7 +112,7 @@ def tile_list_style_modulated_decoder_kernel(
         w1_raw[1, 1] = load_w1(1, 1)
         load_x([2])
         load_x([3, 4])
-        w3_raw = [load_rows("w3_raw_%d" % g, w3[g * PASS : (g + 1) * PASS, :]) for g in range(2)]
+        w3_raw = [load_weight("w3_raw_%d" % g, w3[g * PASS : (g + 1) * PASS, :], pieces=2) for g in range(2)]
         load_x([5])
         bias = held("bias", [P, SLOTS], F32)
         nc.sync.dma_start(bias[:], b3.rearrange("(p t) -> p t", t=SLOTS))
@@ -129,14 +135,13 @@ def tile_list_style_modulated_decoder_kernel(
 
         def round_weight(raw, buffer):
             dealt = held("rounded_%d" % buffer, [P, SLOTS * PASS], BF16)
-            nc.scalar.copy(
-                dealt[:].rearrange("p (u e m j) -> p u m j e", u=2, e=2, j=SLOTS),
-                raw[:].rearrange("p j (m u e) -> p u m j e", u=2, e=2),
-            )
+            by_piece = dealt[:].rearrange("p (u e k m j) -> p k u m j e", u=2, e=2, k=len(raw), j=SLOTS)
+            for k, piece in enumerate(raw):
+                nc.scalar.copy(by_piece[:, k], piece[:].rearrange("p j (m u e) -> p u m j e", u=2, e=2))
             return dealt
 
-        def quantise(name, rounded, width, calls=1):
-            codes = held(name + "_codes", [P, width], U32)
+        def quantise(name, rounded, width, calls=1, buffer=None):
+            codes = held(buffer or name + "_codes", [P, width], U32)
             plane = held(name + "_plane", [P, width], U8)
             each = width // calls
             for lo in range(0, width, each):
@@ -199,7 +204,7 @@ def tile_list_style_modulated_decoder_kernel(
                 )
             return b_bank[:].rearrange("p t c -> p c t")
 
-        parked_tile = held("w1_raw_1_0", [P, len(GPSIMD_STEPS), 2, BLOCK, 2], F32)
+        parked_tile = held("w1_raw_1_0_0", [P, len(GPSIMD_STEPS), 2, BLOCK, 2], F32)
         parked = {}
         for k, step in enumerate(GPSIMD_STEPS):
             parked[step] = parked_tile[:, k]
@@ -218,7 +223,7 @@ def tile_list_style_modulated_decoder_kernel(
                     nc.vector.tensor_tensor(h_block, shift, scaled_block.rearrange("p u c e -> p c u e"), ADD)
             return h_rounded[:].rearrange("p c u e -> p (c u e)")
 
-        y_sb = [held("w1_raw_0_%d" % half, [P, SLOTS, HALF], F32) for half in range(2)]
+        y_sb = [held("w1_raw_0_%d_0" % half, [P, SLOTS, HALF], F32) for half in range(2)]
         y_plane = held("y_plane", [P, S], U8)
         out_rows = out_0.rearrange("(p t) j -> p t j", t=SLOTS)
         out_words = out_1[0].rearrange("p m t -> p (m t)").bitcast(I32)
@@ -228,8 +233,7 @@ def tile_list_style_modulated_decoder_kernel(
         def decode(lo, width):
             half, at = divmod(lo, HALF)
             y_part = y_sb[half][:, :, at : at + width]
-            very_last = lo + width == S
-            per_bank = 2 if very_last else BANK // width
+            per_bank = BANK // width
             for first in range(0, SLOTS, per_bank):
                 if width == BLOCK:
                     y_bank = psum.tile([P, per_bank, width], F32, name="a_bank")
@@ -251,7 +255,7 @@ def tile_list_style_modulated_decoder_kernel(
                             stop=(g == 1 and e == per_bank - 1),
                         )
                 slots = slice(first, first + per_bank)
-                if very_last and first > 0:
+                if lo + width + BLOCK == S:
                     spread = bias[:, slots].unsqueeze(2).to_broadcast([P, per_bank, width])
                     nc.vector.tensor_tensor(y_part[:, slots, :], y_bank[:], spread, ADD)
                 else:
@@ -265,8 +269,8 @@ def tile_list_style_modulated_decoder_kernel(
                     )
             return lo, width, y_part
 
-        def round_y(lo, width, y_part):
-            y_rounded = held("y_rounded_%d" % lo, [P, SLOTS * width], BF16)
+        def round_y(lo, width, y_part, buffer=None):
+            y_rounded = held(buffer or "y_rounded_%d" % lo, [P, SLOTS * width], BF16)
             copy = nc.vector.tensor_copy if lo in ROUNDED_ON_VECTOR else nc.scalar.copy
             copy(
                 y_rounded[:, : SLOTS * width].rearrange("p (c i t) -> p c t i", i=2, t=SLOTS),
@@ -284,8 +288,8 @@ def tile_list_style_modulated_decoder_kernel(
                 )
             nc.sync.dma_start(out_words[:, start:stop], codes[:].bitcast(I32))
 
-        def pack_h(g, lo, width, h_rounded):
-            codes, plane = quantise("h_%d_%d" % (g, lo), h_rounded, width)
+        def pack_h(g, lo, width, h_rounded, buffer=None):
+            codes, plane = quantise("h_%d_%d" % (g, lo), h_rounded, width, buffer=buffer)
             for first in range(lo, lo + width, BLOCK):
                 h_q[g, first] = (codes, plane, lo)
 
@@ -298,35 +302,34 @@ def tile_list_style_modulated_decoder_kernel(
                 w1_q[1, 1] = quantise("w1_1_1", round_weight(w1_raw[1, 1], 3), PASS)
             scaled[step] = ring.tile([P, 2, PAIR, 2], F32, name="scaled", align_bytes=64)
             scale_slots(step, 0, scaled[step])
+            if step >= 1:
+                h_rounded[step - 1] = add_shift(step - 1, scaled[step - 1], H_BUFFERS[step - 1], 0, PAIR)
             if step == 5:
                 w3_q.append(quantise("w3_1", round_weight(w3_raw[1], 1), N))
                 decoded.append(round_y(*decode(STEPS[3][1], PAIR)))
-            if step >= 1:
-                h_rounded[step - 1] = add_shift(step - 1, scaled[step - 1], H_BUFFERS[step - 1], 0, PAIR)
             scale_slots(step, 1, scaled[step])
             if step == 2:
                 w1_q[0, 1] = quantise("w1_0_1", round_weight(w1_raw[0, 1], 2), PASS)
             if step == 4:
                 w3_q.append(quantise("w3_0", round_weight(w3_raw[0], 0), N))
-            for earlier in range(step):
-                if step == earlier + (2 if earlier in parked else 1) and earlier < last - 1:
-                    pack_h(*STEPS[earlier], PAIR, h_rounded[earlier])
-            if step == 6:
+            if 1 <= step < last:
+                pack_h(*STEPS[step - 1], PAIR, h_rounded[step - 1], H_CODE_BUFFERS.get(step - 1))
+            if step == 5:
                 second_pair = decode(STEPS[4][1], PAIR)
+            if step == 6:
                 third_pair = decode(STEPS[5][1], PAIR)
-                decoded.append(round_y(*second_pair))
-        pack_y("y_codes_0", decoded[0])
+                decoded.append(round_y(*second_pair, "h_1_512_codes"))
         g, lo = STEPS[last]
         h_first_block = add_shift(last, scaled[last], "rounded_3", 0, BLOCK)
+        h_second_block = add_shift(last, scaled[last], "rounded_2", BLOCK, PAIR)
         pack_h(*STEPS[last - 1], PAIR, h_rounded[last - 1])
         pack_h(g, lo, BLOCK, h_first_block)
-        first_block = decode(lo, BLOCK)
-        h_second_block = add_shift(last, scaled[last], "rounded_2", BLOCK, PAIR)
-        pack_y("rounded_3", decoded[1])
         pack_h(g, lo + BLOCK, BLOCK, h_second_block)
+        pack_y("h_0", decoded[0])
         decoded.append(round_y(*third_pair))
+        first_block = decode(lo, BLOCK)
         second_block = decode(lo + BLOCK, BLOCK)
-        pack_y("rounded_2", decoded[2])
+        pack_y("rounded_2", decoded[1], decoded[2])
         pack_y("y_codes", round_y(*first_block), round_y(*second_block))
 
         for q in range(4):

@@ -30,9 +30,9 @@ TAB_FIRST_ROW = 4
 STEPS = [(0, 0), (0, 256), (0, 512), (1, 0), (1, 256), (1, 512), (0, 768), (1, 768)]
 Y_STORES = [(0, 256), (256, 512), (512, 768), (768, 896), (896, 1024)]
 ROUNDED_ON_VECTOR = (512, 896)
-GPSIMD_STEPS = (5, 6)
-H_BUFFERS = ["h_0", "h_1", "h_0", "h_1", "h_0", "h_0", "h_0"]
-H_CODE_BUFFERS = {4: "rounded_1"}
+GPSIMD_STEPS = (3, 5, 6)
+H_BUFFERS = ["h_0", "h_1", "h_0", "h_0", "h_1", "h_1", "h_1"]
+H_CODE_BUFFERS = {3: "w3_raw_0_1", 4: "rounded_1"}
 
 
 def tile_list_style_modulated_decoder_kernel(
@@ -235,7 +235,7 @@ def tile_list_style_modulated_decoder_kernel(
             y_part = y_sb[half][:, :, at : at + width]
             per_bank = BANK // width
             for first in range(0, SLOTS, per_bank):
-                if width == BLOCK:
+                if lo + first // per_bank >= STEPS[5][1] and (lo, first) != (STEPS[5][1], per_bank):
                     y_bank = psum.tile([P, per_bank, width], F32, name="a_bank")
                 else:
                     y_bank = psum_y.tile([P, per_bank, width], F32, name="y_bank")
@@ -255,7 +255,7 @@ def tile_list_style_modulated_decoder_kernel(
                             stop=(g == 1 and e == per_bank - 1),
                         )
                 slots = slice(first, first + per_bank)
-                if lo + width + BLOCK == S:
+                if lo + width == S:
                     spread = bias[:, slots].unsqueeze(2).to_broadcast([P, per_bank, width])
                     nc.vector.tensor_tensor(y_part[:, slots, :], y_bank[:], spread, ADD)
                 else:
@@ -314,18 +314,16 @@ def tile_list_style_modulated_decoder_kernel(
                 w3_q.append(quantise("w3_0", round_weight(w3_raw[0], 0), N))
             if 1 <= step < last:
                 pack_h(*STEPS[step - 1], PAIR, h_rounded[step - 1], H_CODE_BUFFERS.get(step - 1))
-            if step == 5:
-                second_pair = decode(STEPS[4][1], PAIR)
-            if step == 6:
-                third_pair = decode(STEPS[5][1], PAIR)
-                decoded.append(round_y(*second_pair, "h_1_512_codes"))
         g, lo = STEPS[last]
+        second_pair = decode(STEPS[4][1], PAIR)
+        third_pair = decode(STEPS[5][1], PAIR)
+        decoded.append(round_y(*second_pair, "h_1_512_codes"))
         h_first_block = add_shift(last, scaled[last], "rounded_3", 0, BLOCK)
-        h_second_block = add_shift(last, scaled[last], "rounded_2", BLOCK, PAIR)
         pack_h(*STEPS[last - 1], PAIR, h_rounded[last - 1])
+        h_second_block = add_shift(last, scaled[last], "rounded_2", BLOCK, PAIR)
         pack_h(g, lo, BLOCK, h_first_block)
         pack_h(g, lo + BLOCK, BLOCK, h_second_block)
-        pack_y("h_0", decoded[0])
+        pack_y("h_1", decoded[0])
         decoded.append(round_y(*third_pair))
         first_block = decode(lo, BLOCK)
         second_block = decode(lo + BLOCK, BLOCK)

@@ -29,10 +29,10 @@ TAB_FIRST_ROW = 4
 
 STEPS = [(0, 0), (0, 256), (0, 512), (1, 0), (1, 256), (1, 512), (0, 768), (1, 768)]
 Y_STORES = [(0, 256), (256, 512), (512, 768), (768, 896), (896, 1024)]
-ROUNDED_ON_VECTOR = (512, 896)
-GPSIMD_STEPS = (3, 5, 6)
-H_BUFFERS = ["h_0", "h_1", "h_0", "h_0", "h_1", "h_1", "h_1"]
-H_CODE_BUFFERS = {3: "w3_raw_0_1", 4: "rounded_1"}
+ROUNDED_ON_VECTOR = (384, 512, 896)
+GPSIMD_STEPS = (2, 3, 5, 6)
+H_BUFFERS = ["h_0", "h_1", "rounded_3", "rounded_3", "h_1", "h_1", "h_1"]
+H_CODE_BUFFERS = {3: "w3_raw_0_1", 4: "rounded_0"}
 
 
 def tile_list_style_modulated_decoder_kernel(
@@ -107,7 +107,7 @@ def tile_list_style_modulated_decoder_kernel(
         load_plane(w2_plane_raw, w2_scales)
         w1_raw[1, 0] = load_w1(1, 0)
         tab.append(load_words("tab_1", tab_words[1], T))
-        load_x([0, 1], parts=2)
+        load_x([0, 1])
         w1_raw[0, 1] = load_w1(0, 1)
         w1_raw[1, 1] = load_w1(1, 1)
         load_x([2])
@@ -233,9 +233,10 @@ def tile_list_style_modulated_decoder_kernel(
         def decode(lo, width):
             half, at = divmod(lo, HALF)
             y_part = y_sb[half][:, :, at : at + width]
-            per_bank = BANK // width
+            very_last = lo + width == S
+            per_bank = 2 if very_last else BANK // width
             for first in range(0, SLOTS, per_bank):
-                if lo + first // per_bank >= STEPS[5][1] and (lo, first) != (STEPS[5][1], per_bank):
+                if lo >= STEPS[5][1] and first == 0:
                     y_bank = psum.tile([P, per_bank, width], F32, name="a_bank")
                 else:
                     y_bank = psum_y.tile([P, per_bank, width], F32, name="y_bank")
@@ -255,7 +256,7 @@ def tile_list_style_modulated_decoder_kernel(
                             stop=(g == 1 and e == per_bank - 1),
                         )
                 slots = slice(first, first + per_bank)
-                if lo + width == S:
+                if very_last and first == 0:
                     spread = bias[:, slots].unsqueeze(2).to_broadcast([P, per_bank, width])
                     nc.vector.tensor_tensor(y_part[:, slots, :], y_bank[:], spread, ADD)
                 else:
@@ -267,9 +268,10 @@ def tile_list_style_modulated_decoder_kernel(
                     nc.sync.dma_start(
                         out_rows[:, :, start:stop], y_sb[half][:, :, start - half * HALF : stop - half * HALF]
                     )
-            return lo, width, y_part
 
-        def round_y(lo, width, y_part, buffer=None):
+        def round_y(lo, width, buffer=None):
+            half, at = divmod(lo, HALF)
+            y_part = y_sb[half][:, :, at : at + width]
             y_rounded = held(buffer or "y_rounded_%d" % lo, [P, SLOTS * width], BF16)
             copy = nc.vector.tensor_copy if lo in ROUNDED_ON_VECTOR else nc.scalar.copy
             copy(
@@ -295,42 +297,48 @@ def tile_list_style_modulated_decoder_kernel(
 
         scaled = {}
         h_rounded = {}
-        decoded = []
         last = len(STEPS) - 1
         for step in range(len(STEPS)):
             if step == 3:
                 w1_q[1, 1] = quantise("w1_1_1", round_weight(w1_raw[1, 1], 3), PASS)
             scaled[step] = ring.tile([P, 2, PAIR, 2], F32, name="scaled", align_bytes=64)
             scale_slots(step, 0, scaled[step])
+            if step == 4:
+                scale_slots(step, 1, scaled[step])
+            if step == last:
+                pack_h(*STEPS[5], PAIR, h_rounded[5])
             if step >= 1:
                 h_rounded[step - 1] = add_shift(step - 1, scaled[step - 1], H_BUFFERS[step - 1], 0, PAIR)
             if step == 5:
                 w3_q.append(quantise("w3_1", round_weight(w3_raw[1], 1), N))
-                decoded.append(round_y(*decode(STEPS[3][1], PAIR)))
-            scale_slots(step, 1, scaled[step])
+                decode(0, PAIR)
+                rounded = [round_y(0, PAIR)]
+            if step != 4:
+                scale_slots(step, 1, scaled[step])
             if step == 2:
                 w1_q[0, 1] = quantise("w1_0_1", round_weight(w1_raw[0, 1], 2), PASS)
             if step == 4:
                 w3_q.append(quantise("w3_0", round_weight(w3_raw[0], 0), N))
-            if 1 <= step < last:
+            if 1 <= step < last - 1:
                 pack_h(*STEPS[step - 1], PAIR, h_rounded[step - 1], H_CODE_BUFFERS.get(step - 1))
         g, lo = STEPS[last]
-        second_pair = decode(STEPS[4][1], PAIR)
-        third_pair = decode(STEPS[5][1], PAIR)
-        decoded.append(round_y(*second_pair, "h_1_512_codes"))
         h_first_block = add_shift(last, scaled[last], "rounded_3", 0, BLOCK)
         pack_h(*STEPS[last - 1], PAIR, h_rounded[last - 1])
         h_second_block = add_shift(last, scaled[last], "rounded_2", BLOCK, PAIR)
+        decode(PAIR, PAIR)
+        decode(2 * PAIR, PAIR)
+        rounded.append(round_y(PAIR, BLOCK, "h_1_512_codes"))
         pack_h(g, lo, BLOCK, h_first_block)
         pack_h(g, lo + BLOCK, BLOCK, h_second_block)
-        pack_y("h_1", decoded[0])
-        decoded.append(round_y(*third_pair))
-        first_block = decode(lo, BLOCK)
-        second_block = decode(lo + BLOCK, BLOCK)
-        pack_y("rounded_2", decoded[1], decoded[2])
-        pack_y("y_codes", round_y(*first_block), round_y(*second_block))
+        rounded.append(round_y(3 * BLOCK, BLOCK, "h_1"))
+        pack_y("rounded_3", *rounded)
+        rounded = [round_y(2 * PAIR, PAIR, "h_1_512_codes")]
+        decode(lo, BLOCK)
+        decode(lo + BLOCK, BLOCK)
+        pack_y("rounded_2", *rounded, round_y(lo, BLOCK), round_y(lo + BLOCK, BLOCK))
 
         for q in range(4):
-            nc.scalar.dma_start(
+            queue = nc.scalar if q < 2 else nc.sync
+            queue.dma_start(
                 out_2[0, 4 * q : 4 * q + 4, :].bitcast(I32), y_plane[32 * q : 32 * q + 4, :].bitcast(I32)
             )

@@ -27,13 +27,6 @@ PAIRS = S // PAIR
 HALF = S // 2
 TAB_FIRST_ROW = 4
 
-STEPS = [(0, 0), (0, 256), (0, 512), (1, 0), (1, 256), (1, 512), (0, 768), (1, 768)]
-Y_STORES = [(0, 256), (256, 512), (512, 768), (768, 896), (896, 1024)]
-ROUNDED_ON_VECTOR = (384, 512, 896)
-GPSIMD_STEPS = (2, 3, 5, 6)
-H_BUFFERS = ["h_0", "h_1", "rounded_3", "rounded_3", "h_1", "h_1", "h_1"]
-H_CODE_BUFFERS = {3: "w3_raw_0_1", 4: "rounded_0"}
-
 
 def tile_list_style_modulated_decoder_kernel(
     tc, tab_words, tab_scales, tab2_words, tab2_scales, offs, offs2, w1, w2_words, w2_scales, x, w3, b3,
@@ -42,12 +35,13 @@ def tile_list_style_modulated_decoder_kernel(
     nc = tc.nc
     with ExitStack() as ctx:
         keep = ctx.enter_context(tc.tile_pool(name="keep", bufs=1))
-        ring = ctx.enter_context(tc.tile_pool(name="ring", bufs=3))
-        psum = ctx.enter_context(tc.psum_pool(name="psum", bufs=3))
-        psum_y = ctx.enter_context(tc.psum_pool(name="psum_y", bufs=2))
+        psum = ctx.enter_context(tc.psum_pool(name="psum", bufs=1))
 
         def held(name, shape, dtype):
             return keep.tile(shape, dtype, name=name, align_bytes=64)
+
+        def bank(number, parts):
+            return psum.tile([P, parts, BANK // parts], F32, name="bank_%d" % number)
 
         w2_plane_raw = held("w2_plane_raw", [P, H], U8)
         tab2_plane = held("tab2_plane", [P, T2], U8)
@@ -70,27 +64,22 @@ def tile_list_style_modulated_decoder_kernel(
             nc.sync.dma_start(tile[:].bitcast(I32), words.rearrange("p n t -> p (n t)").bitcast(I32))
             return tile
 
-        def load_rows(name, rows, parts=1):
-            tile = held(name, [P, SLOTS, rows.shape[1]], F32)
-            by_slot = rows.rearrange("(p t) c -> p t c", t=SLOTS)
-            each = SLOTS // parts
-            for t in range(0, SLOTS, each):
-                nc.sync.dma_start(tile[:, t : t + each, :], by_slot[:, t : t + each, :])
+        def load_rows(name, matrix, g, slots, lo, hi):
+            tile = held(name, [P, len(slots), hi - lo], F32)
+            by_slot = matrix[g * PASS : (g + 1) * PASS, lo:hi].rearrange("(p t) c -> p t c", t=SLOTS)
+            nc.sync.dma_start(tile[:], by_slot[:, slots.start : slots.stop, :])
             return tile
 
-        def load_weight(name, rows, pieces=1):
-            width = PASS // pieces
-            return [load_rows("%s_%d" % (name, k), rows[:, k * width : (k + 1) * width]) for k in range(pieces)]
+        x_sb = {}
 
-        def load_w1(a, g, pieces=1):
-            rows = w1[a * PASS : (a + 1) * PASS, g * PASS : (g + 1) * PASS]
-            return load_weight("w1_raw_%d_%d" % (a, g), rows, pieces)
+        def load_x(g, pairs, lo, hi):
+            tile = load_rows("x_%d_%d_%d" % (g, pairs[0], lo), x, g, range(2 * pairs[0], 2 * pairs[-1] + 2), lo, hi)
+            for k, u in enumerate(pairs):
+                for at in range(lo, hi, PAIR):
+                    x_sb[g, u, at] = tile[:, 2 * k : 2 * k + 2, at - lo : at - lo + PAIR]
 
-        def load_x(steps, parts=1):
-            g, lo = STEPS[steps[0]]
-            tile = load_rows("x_%d" % steps[0], x[g * PASS : (g + 1) * PASS, lo : lo + PAIR * len(steps)], parts)
-            for k, step in enumerate(steps):
-                x_sb[step] = tile[:, :, k * PAIR : (k + 1) * PAIR]
+        def load_w1(a, g):
+            return load_rows("w1_raw_%d_%d" % (a, g), w1, a, range(SLOTS), g * PASS, (g + 1) * PASS)
 
         w2_raw = held("w2_raw", [P, 2 * H], U8)
         nc.sync.dma_start(w2_raw[:].bitcast(I32), w2_words[0].bitcast(I32))
@@ -102,22 +91,21 @@ def tile_list_style_modulated_decoder_kernel(
         list1 = held("list1", [P, S // 16], U16)
         nc.sync.dma_start(list1[:], offs)
         w1_raw = {}
-        x_sb = {}
         w1_raw[0, 0] = load_w1(0, 0)
         load_plane(w2_plane_raw, w2_scales)
         w1_raw[1, 0] = load_w1(1, 0)
         tab.append(load_words("tab_1", tab_words[1], T))
-        load_x([0, 1])
+        load_x(0, [0], 0, S)
+        load_x(0, [1], 0, S)
         w1_raw[0, 1] = load_w1(0, 1)
         w1_raw[1, 1] = load_w1(1, 1)
-        load_x([2])
-        load_x([3, 4])
-        w3_raw = [load_weight("w3_raw_%d" % g, w3[g * PASS : (g + 1) * PASS, :], pieces=2) for g in range(2)]
-        load_x([5])
+        load_x(1, [0], 0, HALF)
+        load_x(1, [1], 0, HALF)
+        w3_raw = [load_rows("w3_raw_%d" % g, w3, g, range(SLOTS), 0, N) for g in range(2)]
         bias = held("bias", [P, SLOTS], F32)
         nc.sync.dma_start(bias[:], b3.rearrange("(p t) -> p t", t=SLOTS))
-        load_x([6])
-        load_x([7])
+        load_x(1, [0, 1], HALF, HALF + PAIR)
+        load_x(1, [0, 1], HALF + PAIR, S)
 
         def gather(name, window, offsets, dtype, parts):
             width = S // parts
@@ -134,22 +122,169 @@ def tile_list_style_modulated_decoder_kernel(
             return tiles[lo // width][first_row:P, lo % width : lo % width + count]
 
         def round_weight(raw, buffer):
-            dealt = held("rounded_%d" % buffer, [P, SLOTS * PASS], BF16)
-            by_piece = dealt[:].rearrange("p (u e k m j) -> p k u m j e", u=2, e=2, k=len(raw), j=SLOTS)
-            for k, piece in enumerate(raw):
-                nc.scalar.copy(by_piece[:, k], piece[:].rearrange("p j (m u e) -> p u m j e", u=2, e=2))
+            dealt = held(buffer, [P, SLOTS * PASS], BF16)
+            nc.scalar.copy(
+                dealt[:].rearrange("p (u e m j) -> p u m j e", u=2, e=2, j=SLOTS),
+                raw[:].rearrange("p j (m u e) -> p u m j e", u=2, e=2),
+            )
             return dealt
 
-        def quantise(name, rounded, width, calls=1, buffer=None):
+        def round_pair(raw, u, buffer, copy=nc.scalar.copy):
+            dealt = held(buffer, [P, 2 * PASS], BF16)
+            copy(
+                dealt[:].rearrange("p (e m j) -> p m j e", e=2, j=SLOTS),
+                raw[:].rearrange("p j (m u e) -> p u m j e", u=2, e=2)[:, u],
+            )
+            return dealt
+
+        def quantise(name, rounded, width, buffer=None):
             codes = held(buffer or name + "_codes", [P, width], U32)
             plane = held(name + "_plane", [P, width], U8)
-            each = width // calls
-            for lo in range(0, width, each):
-                nc.vector.quantize_mx(
-                    codes[:, lo : lo + each].bitcast(E4M3), plane[:, lo : lo + each],
-                    rounded[:, SLOTS * lo : SLOTS * (lo + each)],
-                )
+            nc.vector.quantize_mx(codes[:].bitcast(E4M3), plane[:], rounded[:])
             return codes, plane
+
+        def by_pairs(whole):
+            codes, plane = whole
+            return [(codes[:, u * PAIR : (u + 1) * PAIR], plane[:, u * PAIR : (u + 1) * PAIR]) for u in range(2)]
+
+        w1_q = {}
+        w3_q = {}
+        scaled = {}
+        parked = {}
+        h_rounded = {}
+        h_q = {}
+
+        def scale_slots(g, u, lo, number, buffer=None):
+            a_bank = bank(number, 2)
+            for a in range(2):
+                codes, plane = w1_q[a, g][u]
+                for e in range(2):
+                    places = slice(e * P, (e + 1) * P)
+                    nc.tensor.matmul_mx(
+                        a_bank[:, e, :],
+                        lhsT=codes[:, places].bitcast(E4M3),
+                        lhsT_scale=plane[:, places],
+                        rhs=columns(v_words[a], lo, PAIR).bitcast(E4M3),
+                        rhs_scale=columns(v_plane, lo, PAIR, TAB_FIRST_ROW + 4 * a),
+                        start=(a == 0 and e == 0),
+                        stop=(a == 1 and e == 1),
+                    )
+            if u == 0:
+                scaled[g, lo] = held(buffer or "scaled_%d" % lo, [P, 2, PAIR, 2], F32)
+            nc.vector.scalar_tensor_tensor(
+                scaled[g, lo][:, u], a_bank[:].rearrange("p e c -> p c e"), 1.0,
+                x_sb[g, u, lo].rearrange("p e c -> p c e"), ADD, MULT,
+            )
+
+        def shift_block(g, lo, number):
+            b_bank = bank(number, SLOTS)
+            for t in range(SLOTS):
+                place = g * PASS + t * P
+                nc.tensor.matmul_mx(
+                    b_bank[:, t, :],
+                    lhsT=w2_dealt[:, 2 * place : 2 * (place + P)].bitcast(E2M1),
+                    lhsT_scale=w2_plane[:, place : place + P],
+                    rhs=columns(v2_words, lo, BLOCK).bitcast(E4M3),
+                    rhs_scale=columns(v2_plane, lo, BLOCK),
+                    start=True,
+                    stop=True,
+                )
+            return b_bank[:].rearrange("p t c -> p c t")
+
+        def park(k, g, lo, number):
+            parked[g, lo] = parked_tile[:, k]
+            nc.scalar.copy(parked[g, lo], shift_block(g, lo, number).rearrange("p c (u e) -> p u c e", e=2))
+
+        def h_tile(g, lo, width, buffer=None):
+            tile = held(buffer or "h_%d_%d" % (g, lo), [P, width, 2, 2], BF16)
+            for at in range(lo, lo + width, BLOCK):
+                h_rounded[g, at] = (tile, lo)
+
+        def add_shift(g, lo, number=None):
+            tile, first = h_rounded[g, lo]
+            h_block = tile[:, lo - first : lo - first + BLOCK]
+            at = lo % PAIR
+            scaled_block = scaled[g, lo - at][:, :, at : at + BLOCK, :]
+            if (g, lo) in parked:
+                nc.gpsimd.tensor_tensor(h_block.rearrange("p c u e -> p u c e"), parked[g, lo], scaled_block, ADD)
+            else:
+                shift = shift_block(g, lo, number).rearrange("p c (u e) -> p c u e", e=2)
+                nc.vector.tensor_tensor(h_block, shift, scaled_block.rearrange("p u c e -> p c u e"), ADD)
+
+        def pack_h(g, lo, width, buffer=None):
+            tile, first = h_rounded[g, lo]
+            rounded = tile[:, lo - first : lo - first + width].rearrange("p c u e -> p (c u e)")
+            codes, plane = quantise("h_%d_%d" % (g, lo), rounded, width, buffer)
+            for at in range(lo, lo + width, BLOCK):
+                h_q[g, at] = (codes, plane, lo, lo + width)
+
+        out_rows = out_0.rearrange("(p t) j -> p t j", t=SLOTS)
+        out_words = out_1[0].rearrange("p m t -> p (m t)").bitcast(I32)
+        y_plane = held("y_plane", [P, S], U8)
+        y_sb = {}
+
+        def y_tile(lo, width, buffer):
+            tile = held(buffer, [P, SLOTS, width], F32)
+            for at in range(lo, lo + width, BLOCK):
+                y_sb[at] = (tile, lo)
+
+        def y_part(lo, width):
+            tile, first = y_sb[lo]
+            return tile[:, :, lo - first : lo - first + width]
+
+        def decode(lo, width, slots, number, on_vector=False):
+            y_bank = psum.tile([P, len(slots), width], F32, name="bank_%d" % number)
+            passes = []
+            for g in range(2):
+                for e, t in enumerate(slots):
+                    at = lo
+                    while at < lo + width:
+                        stop = min(h_q[g, at][3], lo + width)
+                        passes.append((g, e, t, at, stop))
+                        at = stop
+            for k, (g, e, t, at, stop) in enumerate(passes):
+                h_codes, h_plane, h_first = h_q[g, at][:3]
+                codes, plane = w3_q[g][t // 2]
+                places = slice(t % 2 * P, (t % 2 + 1) * P)
+                nc.tensor.matmul_mx(
+                    y_bank[:, e, at - lo : stop - lo],
+                    lhsT=codes[:, places].bitcast(E4M3),
+                    lhsT_scale=plane[:, places],
+                    rhs=h_codes[:, at - h_first : stop - h_first].bitcast(E4M3),
+                    rhs_scale=h_plane[:, at - h_first : stop - h_first],
+                    start=(k == 0),
+                    stop=(k == len(passes) - 1),
+                )
+            target = y_part(lo, width)
+            if on_vector:
+                spread = bias[:, slots.start : slots.stop].unsqueeze(2).to_broadcast([P, len(slots), width])
+                nc.vector.tensor_tensor(target[:, slots.start : slots.stop, :], y_bank[:], spread, ADD)
+            else:
+                for e, t in enumerate(slots):
+                    nc.scalar.activation(target[:, t, :], y_bank[:, e, :], IDENTITY, bias=bias[:, t : t + 1])
+
+        def store_y(lo, width, slots):
+            nc.sync.dma_start(
+                out_rows[:, slots.start : slots.stop, lo : lo + width], y_part(lo, width)[:, slots.start : slots.stop, :]
+            )
+
+        def round_y(lo, width, copy, buffer=None):
+            y_rounded = held(buffer or "y_rounded_%d" % lo, [P, SLOTS * width], BF16)
+            copy(
+                y_rounded[:].rearrange("p (c i t) -> p c t i", i=2, t=SLOTS),
+                y_part(lo, width).rearrange("p t (c i) -> p c t i", i=2),
+            )
+            return lo, width, y_rounded
+
+        def pack_y(buffer, *stretches):
+            start = stretches[0][0]
+            stop = stretches[-1][0] + stretches[-1][1]
+            codes = held(buffer, [P, stop - start], U32)
+            for lo, width, y_rounded in stretches:
+                nc.vector.quantize_mx(
+                    codes[:, lo - start : lo - start + width].bitcast(E4M3), y_plane[:, lo : lo + width], y_rounded[:]
+                )
+            nc.sync.dma_start(out_words[:, start:stop], codes[:].bitcast(I32))
 
         w2_dealt = held("w2_dealt", [P, 2 * H], U8)
         nc.vector.tensor_copy(
@@ -165,177 +300,84 @@ def tile_list_style_modulated_decoder_kernel(
             w2_plane_raw[:].rearrange("p (g m t) -> p g t m", g=2, t=SLOTS),
         )
         v_plane = gather("v_plane", tab_plane, list1, U8, 1)
-        w1_q = {}
-        w1_q[0, 0] = quantise("w1_0_0", round_weight(w1_raw[0, 0], 0), PASS)
-        w1_q[1, 0] = quantise("w1_1_0", round_weight(w1_raw[1, 0], 1), PASS)
+        w1_q[0, 0] = by_pairs(quantise("w1_0_0", round_weight(w1_raw[0, 0], "rounded_0"), PASS))
+        w1_q[1, 0] = by_pairs(quantise("w1_1_0", round_weight(w1_raw[1, 0], "rounded_1"), PASS))
         v_words.append(gather("v_words_1", tab[1], list1, U32, 2))
+        parked_tile = held("w1_raw_1_0", [P, 3, 2, BLOCK, 2], F32)
+        park(0, 0, 0, 4)
+        park(1, 0, 256, 5)
+        park(2, 1, 512, 6)
 
-        def scale_slots(step, u, scaled):
-            g, lo = STEPS[step]
-            a_bank = psum.tile([P, 2, PAIR], F32, name="a_bank")
-            for a in range(2):
-                codes, plane = w1_q[a, g]
-                for e in range(2):
-                    places = slice((2 * u + e) * P, (2 * u + e + 1) * P)
-                    nc.tensor.matmul_mx(
-                        a_bank[:, e, :],
-                        lhsT=codes[:, places].bitcast(E4M3),
-                        lhsT_scale=plane[:, places],
-                        rhs=columns(v_words[a], lo, PAIR).bitcast(E4M3),
-                        rhs_scale=columns(v_plane, lo, PAIR, TAB_FIRST_ROW + 4 * a),
-                        start=(a == 0 and e == 0),
-                        stop=(a == 1 and e == 1),
-                    )
-            x_part = x_sb[step][:, 2 * u : 2 * u + 2, :].rearrange("p e c -> p c e")
-            nc.vector.scalar_tensor_tensor(scaled[:, u], a_bank[:].rearrange("p e c -> p c e"), 1.0, x_part, ADD, MULT)
-
-        def shift_block(g, lo):
-            b_bank = psum.tile([P, SLOTS, BLOCK], F32, name="b_bank")
-            for t in range(SLOTS):
-                place = g * PASS + t * P
-                nc.tensor.matmul_mx(
-                    b_bank[:, t, :],
-                    lhsT=w2_dealt[:, 2 * place : 2 * (place + P)].bitcast(E2M1),
-                    lhsT_scale=w2_plane[:, place : place + P],
-                    rhs=columns(v2_words, lo, BLOCK).bitcast(E4M3),
-                    rhs_scale=columns(v2_plane, lo, BLOCK),
-                    start=True,
-                    stop=True,
-                )
-            return b_bank[:].rearrange("p t c -> p c t")
-
-        parked_tile = held("w1_raw_1_0_0", [P, len(GPSIMD_STEPS), 2, BLOCK, 2], F32)
-        parked = {}
-        for k, step in enumerate(GPSIMD_STEPS):
-            parked[step] = parked_tile[:, k]
-            nc.scalar.copy(parked[step], shift_block(*STEPS[step]).rearrange("p c (u e) -> p u c e", e=2))
-
-        def add_shift(step, scaled, buffer, start, stop):
-            g, lo = STEPS[step]
-            h_rounded = held(buffer, [P, stop - start, 2, 2], BF16)
-            for at in range(start, stop, BLOCK):
-                h_block = h_rounded[:, at - start : at - start + BLOCK]
-                scaled_block = scaled[:, :, at : at + BLOCK, :]
-                if at == 0 and step in parked:
-                    nc.gpsimd.tensor_tensor(h_block.rearrange("p c u e -> p u c e"), parked[step], scaled_block, ADD)
-                else:
-                    shift = shift_block(g, lo + at).rearrange("p c (u e) -> p c u e", e=2)
-                    nc.vector.tensor_tensor(h_block, shift, scaled_block.rearrange("p u c e -> p c u e"), ADD)
-            return h_rounded[:].rearrange("p c u e -> p (c u e)")
-
-        y_sb = [held("w1_raw_0_%d_0" % half, [P, SLOTS, HALF], F32) for half in range(2)]
-        y_plane = held("y_plane", [P, S], U8)
-        out_rows = out_0.rearrange("(p t) j -> p t j", t=SLOTS)
-        out_words = out_1[0].rearrange("p m t -> p (m t)").bitcast(I32)
-        h_q = {}
-        w3_q = []
-
-        def decode(lo, width):
-            half, at = divmod(lo, HALF)
-            y_part = y_sb[half][:, :, at : at + width]
-            very_last = lo + width == S
-            per_bank = 2 if very_last else BANK // width
-            for first in range(0, SLOTS, per_bank):
-                if lo >= STEPS[5][1] and first == 0:
-                    y_bank = psum.tile([P, per_bank, width], F32, name="a_bank")
-                else:
-                    y_bank = psum_y.tile([P, per_bank, width], F32, name="y_bank")
-                for g in range(2):
-                    codes, plane = w3_q[g]
-                    h_codes, h_plane, h_first = h_q[g, lo]
-                    in_tile = slice(lo - h_first, lo - h_first + width)
-                    for e in range(per_bank):
-                        places = slice((first + e) * P, (first + e + 1) * P)
-                        nc.tensor.matmul_mx(
-                            y_bank[:, e, :],
-                            lhsT=codes[:, places].bitcast(E4M3),
-                            lhsT_scale=plane[:, places],
-                            rhs=h_codes[:, in_tile].bitcast(E4M3),
-                            rhs_scale=h_plane[:, in_tile],
-                            start=(g == 0 and e == 0),
-                            stop=(g == 1 and e == per_bank - 1),
-                        )
-                slots = slice(first, first + per_bank)
-                if very_last and first == 0:
-                    spread = bias[:, slots].unsqueeze(2).to_broadcast([P, per_bank, width])
-                    nc.vector.tensor_tensor(y_part[:, slots, :], y_bank[:], spread, ADD)
-                else:
-                    for e in range(per_bank):
-                        t = first + e
-                        nc.scalar.activation(y_part[:, t, :], y_bank[:, e, :], IDENTITY, bias=bias[:, t : t + 1])
-            for start, stop in Y_STORES:
-                if stop == lo + width:
-                    nc.sync.dma_start(
-                        out_rows[:, :, start:stop], y_sb[half][:, :, start - half * HALF : stop - half * HALF]
-                    )
-
-        def round_y(lo, width, buffer=None):
-            half, at = divmod(lo, HALF)
-            y_part = y_sb[half][:, :, at : at + width]
-            y_rounded = held(buffer or "y_rounded_%d" % lo, [P, SLOTS * width], BF16)
-            copy = nc.vector.tensor_copy if lo in ROUNDED_ON_VECTOR else nc.scalar.copy
-            copy(
-                y_rounded[:, : SLOTS * width].rearrange("p (c i t) -> p c t i", i=2, t=SLOTS),
-                y_part.rearrange("p t (c i) -> p c t i", i=2),
-            )
-            return lo, width, y_rounded
-
-        def pack_y(buffer, *stretches):
-            start = stretches[0][0]
-            stop = stretches[-1][0] + stretches[-1][1]
-            codes = held(buffer, [P, stop - start], U32)
-            for lo, width, y_rounded in stretches:
-                nc.vector.quantize_mx(
-                    codes[:, lo - start : lo - start + width].bitcast(E4M3), y_plane[:, lo : lo + width], y_rounded[:]
-                )
-            nc.sync.dma_start(out_words[:, start:stop], codes[:].bitcast(I32))
-
-        def pack_h(g, lo, width, h_rounded, buffer=None):
-            codes, plane = quantise("h_%d_%d" % (g, lo), h_rounded, width, buffer=buffer)
-            for first in range(lo, lo + width, BLOCK):
-                h_q[g, first] = (codes, plane, lo)
-
-        scaled = {}
-        h_rounded = {}
-        last = len(STEPS) - 1
-        for step in range(len(STEPS)):
-            if step == 3:
-                w1_q[1, 1] = quantise("w1_1_1", round_weight(w1_raw[1, 1], 3), PASS)
-            scaled[step] = ring.tile([P, 2, PAIR, 2], F32, name="scaled", align_bytes=64)
-            scale_slots(step, 0, scaled[step])
-            if step == 4:
-                scale_slots(step, 1, scaled[step])
-            if step == last:
-                pack_h(*STEPS[5], PAIR, h_rounded[5])
-            if step >= 1:
-                h_rounded[step - 1] = add_shift(step - 1, scaled[step - 1], H_BUFFERS[step - 1], 0, PAIR)
-            if step == 5:
-                w3_q.append(quantise("w3_1", round_weight(w3_raw[1], 1), N))
-                decode(0, PAIR)
-                rounded = [round_y(0, PAIR)]
-            if step != 4:
-                scale_slots(step, 1, scaled[step])
-            if step == 2:
-                w1_q[0, 1] = quantise("w1_0_1", round_weight(w1_raw[0, 1], 2), PASS)
-            if step == 4:
-                w3_q.append(quantise("w3_0", round_weight(w3_raw[0], 0), N))
-            if 1 <= step < last - 1:
-                pack_h(*STEPS[step - 1], PAIR, h_rounded[step - 1], H_CODE_BUFFERS.get(step - 1))
-        g, lo = STEPS[last]
-        h_first_block = add_shift(last, scaled[last], "rounded_3", 0, BLOCK)
-        pack_h(*STEPS[last - 1], PAIR, h_rounded[last - 1])
-        h_second_block = add_shift(last, scaled[last], "rounded_2", BLOCK, PAIR)
-        decode(PAIR, PAIR)
-        decode(2 * PAIR, PAIR)
-        rounded.append(round_y(PAIR, BLOCK, "h_1_512_codes"))
-        pack_h(g, lo, BLOCK, h_first_block)
-        pack_h(g, lo + BLOCK, BLOCK, h_second_block)
-        rounded.append(round_y(3 * BLOCK, BLOCK, "h_1"))
-        pack_y("rounded_3", *rounded)
-        rounded = [round_y(2 * PAIR, PAIR, "h_1_512_codes")]
-        decode(lo, BLOCK)
-        decode(lo + BLOCK, BLOCK)
-        pack_y("rounded_2", *rounded, round_y(lo, BLOCK), round_y(lo + BLOCK, BLOCK))
+        for c in range(4):
+            scale_slots(0, 0, c * PAIR, c)
+        h_tile(0, 0, HALF)
+        h_tile(0, HALF, HALF)
+        scale_slots(0, 1, 0, 7)
+        add_shift(0, 0)
+        scale_slots(0, 1, 256, 0)
+        add_shift(0, 256)
+        add_shift(0, 128, 4)
+        scale_slots(0, 1, 512, 1)
+        add_shift(0, 384, 5)
+        scale_slots(0, 1, 768, 2)
+        add_shift(0, 512, 6)
+        add_shift(0, 640, 3)
+        pack_h(0, 0, HALF)
+        w1_q[0, 1] = by_pairs(quantise("w1_0_1", round_weight(w1_raw[0, 1], "rounded_0"), PASS))
+        add_shift(0, 768, 4)
+        add_shift(0, 896, 5)
+        w1_q[1, 1] = [quantise("w1_1_1_0", round_pair(w1_raw[1, 1], 0, "rounded_1"), PAIR)]
+        pack_h(0, HALF, HALF)
+        w1_q[1, 1].append(quantise("w1_1_1_1", round_pair(w1_raw[1, 1], 1, "rounded_2"), PAIR))
+        scale_slots(1, 0, 0, 7)
+        scale_slots(1, 0, 256, 0)
+        h_tile(1, 0, HALF)
+        scale_slots(1, 1, 0, 1)
+        scale_slots(1, 1, 256, 2)
+        add_shift(1, 0, 6)
+        add_shift(1, 128, 3)
+        add_shift(1, 256, 4)
+        add_shift(1, 384, 5)
+        pack_h(1, 0, PAIR)
+        w3_q[0] = by_pairs(quantise("w3_0", round_weight(w3_raw[0], "rounded_0"), PASS))
+        w3_q[1] = [quantise("w3_1_0", round_pair(w3_raw[1], 0, "rounded_1"), PAIR)]
+        pack_h(1, PAIR, PAIR, "rounded_0")
+        scale_slots(1, 0, 512, 2, "rounded_1")
+        scale_slots(1, 1, 512, 6)
+        w3_q[1].append(quantise("w3_1_1", round_pair(w3_raw[1], 1, "rounded_2"), PAIR))
+        y_tile(0, HALF, "w1_raw_0_0")
+        decode(0, HALF, range(0, 1), 7)
+        store_y(0, HALF, range(0, 1))
+        decode(0, HALF, range(1, 2), 0)
+        store_y(0, HALF, range(1, 2))
+        decode(0, HALF, range(2, 3), 2)
+        decode(0, HALF, range(3, 4), 6)
+        store_y(0, HALF, range(2, 4))
+        h_tile(1, 512, PAIR, "rounded_2")
+        add_shift(1, 512)
+        scale_slots(1, 0, 768, 3)
+        add_shift(1, 640, 4)
+        scale_slots(1, 1, 768, 5)
+        pack_h(1, 512, PAIR)
+        h_tile(1, 768, BLOCK)
+        h_tile(1, 896, BLOCK)
+        add_shift(1, 768, 1)
+        add_shift(1, 896, 3)
+        rounded = [round_y(0, PAIR, nc.scalar.copy)]
+        y_tile(HALF, HALF, "w1_raw_0_1")
+        decode(512, PAIR, range(0, 2), 7)
+        store_y(512, PAIR, range(0, 2))
+        decode(512, PAIR, range(2, 4), 0)
+        store_y(512, PAIR, range(2, 4))
+        pack_h(1, 768, BLOCK)
+        pack_h(1, 896, BLOCK)
+        rounded.append(round_y(PAIR, PAIR, nc.vector.tensor_copy, "h_1_896"))
+        decode(768, BLOCK, range(0, 4), 4, on_vector=True)
+        decode(896, BLOCK, range(0, 4), 5)
+        store_y(768, PAIR, range(0, 4))
+        pack_y("y_codes_0", *rounded)
+        rounded = [round_y(512, PAIR, nc.vector.tensor_copy)]
+        pack_y("y_codes_1", *rounded, round_y(768, BLOCK, nc.vector.tensor_copy), round_y(896, BLOCK, nc.scalar.copy))
 
         for q in range(4):
             queue = nc.scalar if q < 2 else nc.sync

@@ -191,9 +191,13 @@ def tile_list_style_modulated_decoder_kernel(
                 )
             return b_bank[:].rearrange("p t c -> p c t")
 
-        def park(k, g, lo, number):
-            parked[g, lo] = parked_tile[:, k]
-            nc.scalar.copy(parked[g, lo], shift_block(g, lo, number).rearrange("p c (u e) -> p u c e", e=2))
+        def park(place, g, lo, number):
+            parked[g, lo] = place
+            nc.scalar.copy(place, shift_block(g, lo, number).rearrange("p c (u e) -> p u c e", e=2))
+
+        def add_pair(g, lo, u, shift):
+            tile, first = h_rounded[g, lo]
+            nc.gpsimd.tensor_tensor(tile[:, lo - first : lo - first + PAIR, u, :], shift[:, u], scaled[g, lo][:, u], ADD)
 
         def h_tile(g, lo, width, buffer=None):
             tile = held(buffer or "h_%d_%d" % (g, lo), [P, width, 2, 2], BF16)
@@ -303,67 +307,75 @@ def tile_list_style_modulated_decoder_kernel(
         w1_q[0, 0] = by_pairs(quantise("w1_0_0", round_weight(w1_raw[0, 0], "rounded_0"), PASS))
         w1_q[1, 0] = by_pairs(quantise("w1_1_0", round_weight(w1_raw[1, 0], "rounded_1"), PASS))
         v_words.append(gather("v_words_1", tab[1], list1, U32, 2))
-        parked_tile = held("w1_raw_1_0", [P, 3, 2, BLOCK, 2], F32)
-        park(0, 0, 0, 4)
-        park(1, 0, 256, 5)
-        park(2, 1, 512, 6)
+        parked_tile = held("w1_raw_1_0", [P, 4, 2, BLOCK, 2], F32)
+        parked_pair = held("rounded_1", [P, 2, PAIR, 2], F32)
+        park(parked_pair[:, :, :BLOCK], 0, 0, 4)
+        park(parked_pair[:, :, BLOCK:], 0, 128, 5)
+        park(parked_tile[:, 0], 0, 256, 6)
+        park(parked_tile[:, 1], 0, 768, 4)
+        park(parked_tile[:, 2], 1, 0, 5)
+        park(parked_tile[:, 3], 0, 896, 6)
 
-        for c in range(4):
-            scale_slots(0, 0, c * PAIR, c)
         h_tile(0, 0, HALF)
-        h_tile(0, HALF, HALF)
+        h_tile(0, HALF, PAIR)
+        scale_slots(0, 0, 0, 0)
+        add_pair(0, 0, 0, parked_pair)
+        for c in range(1, 4):
+            scale_slots(0, 0, c * PAIR, c)
         scale_slots(0, 1, 0, 7)
-        add_shift(0, 0)
+        add_pair(0, 0, 1, parked_pair)
         scale_slots(0, 1, 256, 0)
         add_shift(0, 256)
-        add_shift(0, 128, 4)
         scale_slots(0, 1, 512, 1)
-        add_shift(0, 384, 5)
         scale_slots(0, 1, 768, 2)
-        add_shift(0, 512, 6)
-        add_shift(0, 640, 3)
-        pack_h(0, 0, HALF)
+        add_shift(0, 384, 4)
+        add_shift(0, 512, 5)
+        add_shift(0, 640, 6)
         w1_q[0, 1] = by_pairs(quantise("w1_0_1", round_weight(w1_raw[0, 1], "rounded_0"), PASS))
-        add_shift(0, 768, 4)
-        add_shift(0, 896, 5)
-        w1_q[1, 1] = [quantise("w1_1_1_0", round_pair(w1_raw[1, 1], 0, "rounded_1"), PAIR)]
-        pack_h(0, HALF, HALF)
+        pack_h(0, HALF, PAIR, "rounded_0")
+        w1_q[1, 1] = [quantise("w1_1_1_0", round_pair(w1_raw[1, 1], 0, "rounded_3"), PAIR)]
+        pack_h(0, 0, HALF, "rounded_3")
         w1_q[1, 1].append(quantise("w1_1_1_1", round_pair(w1_raw[1, 1], 1, "rounded_2"), PAIR))
+        h_tile(0, 768, BLOCK, "rounded_2")
+        add_shift(0, 768)
         scale_slots(1, 0, 0, 7)
         scale_slots(1, 0, 256, 0)
         h_tile(1, 0, HALF)
         scale_slots(1, 1, 0, 1)
-        scale_slots(1, 1, 256, 2)
-        add_shift(1, 0, 6)
-        add_shift(1, 128, 3)
-        add_shift(1, 256, 4)
-        add_shift(1, 384, 5)
-        pack_h(1, 0, PAIR)
-        w3_q[0] = by_pairs(quantise("w3_0", round_weight(w3_raw[0], "rounded_0"), PASS))
+        add_shift(1, 0)
+        scale_slots(1, 1, 256, 3)
+        add_shift(1, 128, 4)
+        add_shift(1, 256, 5)
+        add_shift(1, 384, 6)
+        w3_q[0] = by_pairs(quantise("w3_0", round_weight(w3_raw[0], "rounded_4"), PASS))
+        pack_h(1, 0, HALF)
         w3_q[1] = [quantise("w3_1_0", round_pair(w3_raw[1], 0, "rounded_1"), PAIR)]
-        pack_h(1, PAIR, PAIR, "rounded_0")
-        scale_slots(1, 0, 512, 2, "rounded_1")
-        scale_slots(1, 1, 512, 6)
-        w3_q[1].append(quantise("w3_1_1", round_pair(w3_raw[1], 1, "rounded_2"), PAIR))
+        pack_h(0, 768, BLOCK)
+        scale_slots(1, 0, 512, 3, "rounded_1")
+        w3_q[1].append(quantise("w3_1_1", round_pair(w3_raw[1], 1, "rounded_5"), PAIR))
+        h_tile(0, 896, BLOCK, "rounded_5")
+        add_shift(0, 896)
+        scale_slots(1, 1, 512, 4)
         y_tile(0, HALF, "w1_raw_0_0")
         decode(0, HALF, range(0, 1), 7)
         store_y(0, HALF, range(0, 1))
         decode(0, HALF, range(1, 2), 0)
         store_y(0, HALF, range(1, 2))
-        decode(0, HALF, range(2, 3), 2)
-        decode(0, HALF, range(3, 4), 6)
+        decode(0, HALF, range(2, 3), 3)
+        decode(0, HALF, range(3, 4), 4)
         store_y(0, HALF, range(2, 4))
-        h_tile(1, 512, PAIR, "rounded_2")
-        add_shift(1, 512)
-        scale_slots(1, 0, 768, 3)
-        add_shift(1, 640, 4)
-        scale_slots(1, 1, 768, 5)
+        h_tile(1, 512, PAIR)
+        scale_slots(1, 0, 768, 5, "scaled_0")
+        add_shift(1, 512, 2)
+        add_shift(1, 640, 1)
+        scale_slots(1, 1, 768, 6)
         pack_h(1, 512, PAIR)
+        pack_h(0, 896, BLOCK)
         h_tile(1, 768, BLOCK)
         h_tile(1, 896, BLOCK)
-        add_shift(1, 768, 1)
-        add_shift(1, 896, 3)
-        rounded = [round_y(0, PAIR, nc.scalar.copy)]
+        add_shift(1, 768, 5)
+        add_shift(1, 896, 2)
+        rounded = [round_y(0, PAIR, nc.scalar.copy), round_y(256, BLOCK, nc.scalar.copy)]
         y_tile(HALF, HALF, "w1_raw_0_1")
         decode(512, PAIR, range(0, 2), 7)
         store_y(512, PAIR, range(0, 2))
@@ -371,13 +383,13 @@ def tile_list_style_modulated_decoder_kernel(
         store_y(512, PAIR, range(2, 4))
         pack_h(1, 768, BLOCK)
         pack_h(1, 896, BLOCK)
-        rounded.append(round_y(PAIR, PAIR, nc.vector.tensor_copy, "h_1_896"))
-        decode(768, BLOCK, range(0, 4), 4, on_vector=True)
-        decode(896, BLOCK, range(0, 4), 5)
+        rounded.append(round_y(384, BLOCK, nc.vector.tensor_copy, "h_1_768"))
+        pack_y("h_1_896", *rounded)
+        decode(768, BLOCK, range(0, 4), 3)
+        decode(896, BLOCK, range(0, 4), 4, on_vector=True)
         store_y(768, PAIR, range(0, 4))
-        pack_y("y_codes_0", *rounded)
-        rounded = [round_y(512, PAIR, nc.vector.tensor_copy)]
-        pack_y("y_codes_1", *rounded, round_y(768, BLOCK, nc.vector.tensor_copy), round_y(896, BLOCK, nc.scalar.copy))
+        rounded = [round_y(512, BLOCK, nc.scalar.copy), round_y(640, BLOCK, nc.vector.tensor_copy)]
+        pack_y("y_codes_1", *rounded, round_y(768, BLOCK, nc.scalar.copy), round_y(896, BLOCK, nc.vector.tensor_copy))
 
         for q in range(4):
             queue = nc.scalar if q < 2 else nc.sync

@@ -91,8 +91,8 @@ def tile_list_style_modulated_decoder_kernel(
         list1 = held("list1", [P, S // 16], U16)
         nc.sync.dma_start(list1[:], offs)
         w1_raw = {}
-        w1_raw[0, 0] = load_w1(0, 0)
         load_plane(w2_plane_raw, w2_scales)
+        w1_raw[0, 0] = load_w1(0, 0)
         w1_raw[1, 0] = load_w1(1, 0)
         tab.append(load_words("tab_1", tab_words[1], T))
         load_x(0, [0], 0, S)
@@ -107,11 +107,11 @@ def tile_list_style_modulated_decoder_kernel(
         load_x(1, [0, 1], HALF, HALF + PAIR)
         load_x(1, [0, 1], HALF + PAIR, S)
 
-        def gather(name, window, offsets, dtype, parts):
+        def gather(name, window, offsets, dtype, parts, buffer=None):
             width = S // parts
             tiles = []
             for part in range(parts):
-                picked = held("%s_%d" % (name, part), [P, width], dtype)
+                picked = held(buffer or "%s_%d" % (name, part), [P, width], dtype)
                 entries = offsets[:, part * width // 16 : (part + 1) * width // 16]
                 nc.vector.tensor_copy(picked[:], window[:].indirect(entries))
                 tiles.append(picked)
@@ -303,18 +303,18 @@ def tile_list_style_modulated_decoder_kernel(
             w2_plane[:].rearrange("p (g t m) -> p g t m", g=2, t=SLOTS),
             w2_plane_raw[:].rearrange("p (g m t) -> p g t m", g=2, t=SLOTS),
         )
-        v_plane = gather("v_plane", tab_plane, list1, U8, 1)
+        v_plane = gather("v_plane", tab_plane, list1, U8, 1, "w2_plane_raw")
         w1_q[0, 0] = by_pairs(quantise("w1_0_0", round_weight(w1_raw[0, 0], "rounded_0"), PASS))
         w1_q[1, 0] = by_pairs(quantise("w1_1_0", round_weight(w1_raw[1, 0], "rounded_1"), PASS))
         v_words.append(gather("v_words_1", tab[1], list1, U32, 2))
-        parked_tile = held("w1_raw_1_0", [P, 4, 2, BLOCK, 2], F32)
-        parked_pair = held("rounded_1", [P, 2, PAIR, 2], F32)
+        parked_pair = held("w1_raw_0_0", [P, 2, PAIR, 2], F32)
         park(parked_pair[:, :, :BLOCK], 0, 0, 4)
         park(parked_pair[:, :, BLOCK:], 0, 128, 5)
+        parked_tile = held("w1_raw_1_0", [P, 4, 2, BLOCK, 2], F32)
         park(parked_tile[:, 0], 0, 256, 6)
-        park(parked_tile[:, 1], 0, 768, 4)
-        park(parked_tile[:, 2], 1, 0, 5)
-        park(parked_tile[:, 3], 0, 896, 6)
+        park(parked_tile[:, 1], 0, 768, 7)
+        park(parked_tile[:, 2], 1, 0, 4)
+        park(parked_tile[:, 3], 0, 896, 5)
 
         h_tile(0, 0, HALF)
         h_tile(0, HALF, PAIR)
@@ -326,11 +326,11 @@ def tile_list_style_modulated_decoder_kernel(
         add_pair(0, 0, 1, parked_pair)
         scale_slots(0, 1, 256, 0)
         add_shift(0, 256)
-        scale_slots(0, 1, 512, 1)
-        scale_slots(0, 1, 768, 2)
-        add_shift(0, 384, 4)
-        add_shift(0, 512, 5)
-        add_shift(0, 640, 6)
+        scale_slots(0, 1, 512, 3)
+        scale_slots(0, 1, 768, 7)
+        add_shift(0, 384, 0)
+        add_shift(0, 512, 3)
+        add_shift(0, 640, 7)
         w1_q[0, 1] = by_pairs(quantise("w1_0_1", round_weight(w1_raw[0, 1], "rounded_0"), PASS))
         pack_h(0, HALF, PAIR, "rounded_0")
         w1_q[1, 1] = [quantise("w1_1_1_0", round_pair(w1_raw[1, 1], 0, "rounded_3"), PAIR)]
@@ -338,55 +338,55 @@ def tile_list_style_modulated_decoder_kernel(
         w1_q[1, 1].append(quantise("w1_1_1_1", round_pair(w1_raw[1, 1], 1, "rounded_2"), PAIR))
         h_tile(0, 768, BLOCK, "rounded_2")
         add_shift(0, 768)
-        scale_slots(1, 0, 0, 7)
-        scale_slots(1, 0, 256, 0)
+        scale_slots(1, 0, 0, 1)
+        scale_slots(1, 0, 256, 2)
         h_tile(1, 0, HALF)
-        scale_slots(1, 1, 0, 1)
+        scale_slots(1, 1, 0, 5)
         add_shift(1, 0)
-        scale_slots(1, 1, 256, 3)
-        add_shift(1, 128, 4)
-        add_shift(1, 256, 5)
-        add_shift(1, 384, 6)
+        scale_slots(1, 1, 256, 6)
+        add_shift(1, 128, 0)
+        add_shift(1, 256, 3)
+        add_shift(1, 384, 7)
         w3_q[0] = by_pairs(quantise("w3_0", round_weight(w3_raw[0], "rounded_4"), PASS))
         pack_h(1, 0, HALF)
         w3_q[1] = [quantise("w3_1_0", round_pair(w3_raw[1], 0, "rounded_1"), PAIR)]
         pack_h(0, 768, BLOCK)
-        scale_slots(1, 0, 512, 3, "rounded_1")
+        scale_slots(1, 0, 512, 5, "rounded_1")
         w3_q[1].append(quantise("w3_1_1", round_pair(w3_raw[1], 1, "rounded_5"), PAIR))
         h_tile(0, 896, BLOCK, "rounded_5")
         add_shift(0, 896)
-        scale_slots(1, 1, 512, 4)
+        scale_slots(1, 1, 512, 0)
         y_tile(0, HALF, "w1_raw_0_0")
-        decode(0, HALF, range(0, 1), 7)
+        decode(0, HALF, range(0, 1), 1)
         store_y(0, HALF, range(0, 1))
-        decode(0, HALF, range(1, 2), 0)
+        decode(0, HALF, range(1, 2), 6)
         store_y(0, HALF, range(1, 2))
-        decode(0, HALF, range(2, 3), 3)
-        decode(0, HALF, range(3, 4), 4)
+        decode(0, HALF, range(2, 3), 5)
+        decode(0, HALF, range(3, 4), 0)
         store_y(0, HALF, range(2, 4))
         h_tile(1, 512, PAIR)
-        scale_slots(1, 0, 768, 5, "scaled_0")
-        add_shift(1, 512, 2)
-        add_shift(1, 640, 1)
-        scale_slots(1, 1, 768, 6)
+        scale_slots(1, 0, 768, 3, "scaled_0")
+        add_shift(1, 512, 4)
+        add_shift(1, 640, 2)
+        scale_slots(1, 1, 768, 7)
         pack_h(1, 512, PAIR)
         pack_h(0, 896, BLOCK)
         h_tile(1, 768, BLOCK)
         h_tile(1, 896, BLOCK)
-        add_shift(1, 768, 5)
-        add_shift(1, 896, 2)
+        add_shift(1, 768, 3)
+        add_shift(1, 896, 4)
         rounded = [round_y(0, PAIR, nc.scalar.copy), round_y(256, BLOCK, nc.scalar.copy)]
         y_tile(HALF, HALF, "w1_raw_0_1")
-        decode(512, PAIR, range(0, 2), 7)
+        decode(512, PAIR, range(0, 2), 1)
         store_y(512, PAIR, range(0, 2))
-        decode(512, PAIR, range(2, 4), 0)
+        decode(512, PAIR, range(2, 4), 6)
         store_y(512, PAIR, range(2, 4))
         pack_h(1, 768, BLOCK)
         pack_h(1, 896, BLOCK)
         rounded.append(round_y(384, BLOCK, nc.vector.tensor_copy, "h_1_768"))
         pack_y("h_1_896", *rounded)
-        decode(768, BLOCK, range(0, 4), 3)
-        decode(896, BLOCK, range(0, 4), 4, on_vector=True)
+        decode(768, BLOCK, range(0, 4), 5)
+        decode(896, BLOCK, range(0, 4), 0, on_vector=True)
         store_y(768, PAIR, range(0, 4))
         rounded = [round_y(512, BLOCK, nc.scalar.copy), round_y(640, BLOCK, nc.vector.tensor_copy)]
         pack_y("y_codes_1", *rounded, round_y(768, BLOCK, nc.scalar.copy), round_y(896, BLOCK, nc.vector.tensor_copy))

@@ -75,11 +75,18 @@ def tile_list_style_modulated_decoder_kernel(
         def load_x(g, pairs, lo, hi):
             tile = load_rows("x_%d_%d_%d" % (g, pairs[0], lo), x, g, range(2 * pairs[0], 2 * pairs[-1] + 2), lo, hi)
             for k, u in enumerate(pairs):
-                for at in range(lo, hi, PAIR):
-                    x_sb[g, u, at] = tile[:, 2 * k : 2 * k + 2, at - lo : at - lo + PAIR]
+                for at in range(lo, hi, BLOCK):
+                    x_sb[g, u, at] = tile[:, 2 * k : 2 * k + 2, at - lo :]
 
-        def load_w1(a, g):
-            return load_rows("w1_raw_%d_%d" % (a, g), w1, a, range(SLOTS), g * PASS, (g + 1) * PASS)
+        def load_weight(name, matrix, g, first, pieces=1):
+            width = PASS // pieces
+            return [
+                load_rows(name + "_%d" % k * (k > 0), matrix, g, range(SLOTS), first + k * width, first + (k + 1) * width)
+                for k in range(pieces)
+            ]
+
+        def load_w1(a, g, pieces=1):
+            return load_weight("w1_raw_%d_%d" % (a, g), w1, a, g * PASS, pieces)
 
         w2_raw = held("w2_raw", [P, 2 * H], U8)
         nc.sync.dma_start(w2_raw[:].bitcast(I32), w2_words[0].bitcast(I32))
@@ -97,14 +104,13 @@ def tile_list_style_modulated_decoder_kernel(
         tab.append(load_words("tab_1", tab_words[1], T))
         load_x(0, [0], 0, S)
         load_x(0, [1], 0, S)
-        w1_raw[0, 1] = load_w1(0, 1)
-        w1_raw[1, 1] = load_w1(1, 1)
-        load_x(1, [0], 0, HALF)
-        load_x(1, [1], 0, HALF)
-        w3_raw = [load_rows("w3_raw_%d" % g, w3, g, range(SLOTS), 0, N) for g in range(2)]
+        w1_raw[0, 1] = load_w1(0, 1, pieces=2)
+        w1_raw[1, 1] = load_w1(1, 1, pieces=2)
         bias = held("bias", [P, SLOTS], F32)
         nc.sync.dma_start(bias[:], b3.rearrange("(p t) -> p t", t=SLOTS))
-        load_x(1, [0, 1], HALF, HALF + PAIR)
+        load_x(1, [0], 0, 3 * PAIR)
+        load_x(1, [1], 0, 3 * PAIR)
+        w3_raw = [load_weight("w3_raw_%d" % g, w3, g, 0, pieces=2) for g in range(2)]
         load_x(1, [0, 1], HALF + PAIR, S)
 
         def gather(name, window, offsets, dtype, parts, buffer=None):
@@ -123,18 +129,19 @@ def tile_list_style_modulated_decoder_kernel(
 
         def round_weight(raw, buffer):
             dealt = held(buffer, [P, SLOTS * PASS], BF16)
-            nc.scalar.copy(
-                dealt[:].rearrange("p (u e m j) -> p u m j e", u=2, e=2, j=SLOTS),
-                raw[:].rearrange("p j (m u e) -> p u m j e", u=2, e=2),
-            )
+            by_piece = dealt[:].rearrange("p (u e k m j) -> p k u m j e", u=2, e=2, k=len(raw), j=SLOTS)
+            for k, piece in enumerate(raw):
+                nc.scalar.copy(by_piece[:, k], piece[:].rearrange("p j (m u e) -> p u m j e", u=2, e=2))
             return dealt
 
-        def round_pair(raw, u, buffer, copy=nc.scalar.copy):
-            dealt = held(buffer, [P, 2 * PASS], BF16)
-            copy(
-                dealt[:].rearrange("p (e m j) -> p m j e", e=2, j=SLOTS),
-                raw[:].rearrange("p j (m u e) -> p u m j e", u=2, e=2)[:, u],
-            )
+        def round_pairs(raw, buffers):
+            dealt = [held(buffer, [P, 2 * PASS], BF16) for buffer in buffers]
+            for k, piece in enumerate(raw):
+                for u in range(2):
+                    nc.scalar.copy(
+                        dealt[u][:].rearrange("p (e k m j) -> p k m j e", e=2, k=len(raw), j=SLOTS)[:, k],
+                        piece[:].rearrange("p j (m u e) -> p u m j e", u=2, e=2)[:, u],
+                    )
             return dealt
 
         def quantise(name, rounded, width, buffer=None):
@@ -154,8 +161,8 @@ def tile_list_style_modulated_decoder_kernel(
         h_rounded = {}
         h_q = {}
 
-        def scale_slots(g, u, lo, number, buffer=None):
-            a_bank = bank(number, 2)
+        def scale_slots(g, u, lo, number, buffer=None, width=PAIR):
+            a_bank = psum.tile([P, 2, width], F32, name="bank_%d" % number)
             for a in range(2):
                 codes, plane = w1_q[a, g][u]
                 for e in range(2):
@@ -164,16 +171,18 @@ def tile_list_style_modulated_decoder_kernel(
                         a_bank[:, e, :],
                         lhsT=codes[:, places].bitcast(E4M3),
                         lhsT_scale=plane[:, places],
-                        rhs=columns(v_words[a], lo, PAIR).bitcast(E4M3),
-                        rhs_scale=columns(v_plane, lo, PAIR, TAB_FIRST_ROW + 4 * a),
+                        rhs=columns(v_words[a], lo, width).bitcast(E4M3),
+                        rhs_scale=columns(v_plane, lo, width, TAB_FIRST_ROW + 4 * a),
                         start=(a == 0 and e == 0),
                         stop=(a == 1 and e == 1),
                     )
             if u == 0:
-                scaled[g, lo] = held(buffer or "scaled_%d" % lo, [P, 2, PAIR, 2], F32)
+                tile = held(buffer or "scaled_%d" % lo, [P, 2, width, 2], F32)
+                for at in range(0, width, BLOCK):
+                    scaled[g, lo + at] = tile[:, :, at:, :]
             nc.vector.scalar_tensor_tensor(
                 scaled[g, lo][:, u], a_bank[:].rearrange("p e c -> p c e"), 1.0,
-                x_sb[g, u, lo].rearrange("p e c -> p c e"), ADD, MULT,
+                x_sb[g, u, lo][:, :, :width].rearrange("p e c -> p c e"), ADD, MULT,
             )
 
         def shift_block(g, lo, number):
@@ -207,8 +216,7 @@ def tile_list_style_modulated_decoder_kernel(
         def add_shift(g, lo, number=None):
             tile, first = h_rounded[g, lo]
             h_block = tile[:, lo - first : lo - first + BLOCK]
-            at = lo % PAIR
-            scaled_block = scaled[g, lo - at][:, :, at : at + BLOCK, :]
+            scaled_block = scaled[g, lo][:, :, :BLOCK, :]
             if (g, lo) in parked:
                 nc.gpsimd.tensor_tensor(h_block.rearrange("p c u e -> p u c e"), parked[g, lo], scaled_block, ADD)
             else:
@@ -307,89 +315,90 @@ def tile_list_style_modulated_decoder_kernel(
         w1_q[0, 0] = by_pairs(quantise("w1_0_0", round_weight(w1_raw[0, 0], "rounded_0"), PASS))
         w1_q[1, 0] = by_pairs(quantise("w1_1_0", round_weight(w1_raw[1, 0], "rounded_1"), PASS))
         v_words.append(gather("v_words_1", tab[1], list1, U32, 2))
-        parked_pair = held("w1_raw_0_0", [P, 2, PAIR, 2], F32)
-        park(parked_pair[:, :, :BLOCK], 0, 0, 4)
-        park(parked_pair[:, :, BLOCK:], 0, 128, 5)
-        parked_tile = held("w1_raw_1_0", [P, 4, 2, BLOCK, 2], F32)
-        park(parked_tile[:, 0], 0, 256, 6)
-        park(parked_tile[:, 1], 0, 768, 7)
-        park(parked_tile[:, 2], 1, 0, 4)
-        park(parked_tile[:, 3], 0, 896, 5)
+        first_pair = held("w1_raw_0_0", [P, 2, PAIR, 2], F32)
+        park(first_pair[:, :, :BLOCK], 0, 0, 4)
+        park(first_pair[:, :, BLOCK:], 0, 128, 5)
+        parked_tile = held("w1_raw_1_0", [P, 2, 2, PAIR, 2], F32)
+        second_pair = parked_tile[:, 0]
+        park(second_pair[:, :, :BLOCK], 0, 256, 6)
+        park(second_pair[:, :, BLOCK:], 0, 384, 7)
+        third_pair = parked_tile[:, 1]
+        park(third_pair[:, :, :BLOCK], 1, 0, 4)
+        park(third_pair[:, :, BLOCK:], 1, 128, 5)
 
         h_tile(0, 0, HALF)
-        h_tile(0, HALF, PAIR)
+        h_tile(0, HALF, HALF)
         scale_slots(0, 0, 0, 0)
-        add_pair(0, 0, 0, parked_pair)
-        for c in range(1, 4):
-            scale_slots(0, 0, c * PAIR, c)
+        add_pair(0, 0, 0, first_pair)
+        scale_slots(0, 0, 256, 1)
+        add_pair(0, 256, 0, second_pair)
+        scale_slots(0, 0, 512, 2)
+        scale_slots(0, 0, 768, 3)
         scale_slots(0, 1, 0, 7)
-        add_pair(0, 0, 1, parked_pair)
+        add_pair(0, 0, 1, first_pair)
         scale_slots(0, 1, 256, 0)
-        add_shift(0, 256)
+        add_pair(0, 256, 1, second_pair)
         scale_slots(0, 1, 512, 3)
         scale_slots(0, 1, 768, 7)
-        add_shift(0, 384, 0)
-        add_shift(0, 512, 3)
-        add_shift(0, 640, 7)
+        add_shift(0, 512, 0)
+        add_shift(0, 640, 3)
+        add_shift(0, 768, 7)
+        add_shift(0, 896, 0)
+        pack_h(0, HALF, HALF)
         w1_q[0, 1] = by_pairs(quantise("w1_0_1", round_weight(w1_raw[0, 1], "rounded_0"), PASS))
-        pack_h(0, HALF, PAIR, "rounded_0")
-        w1_q[1, 1] = [quantise("w1_1_1_0", round_pair(w1_raw[1, 1], 0, "rounded_3"), PAIR)]
+        rounded = round_pairs(w1_raw[1, 1], ["rounded_3", "rounded_2"])
+        w1_q[1, 1] = [quantise("w1_1_1_0", rounded[0], PAIR)]
         pack_h(0, 0, HALF, "rounded_3")
-        w1_q[1, 1].append(quantise("w1_1_1_1", round_pair(w1_raw[1, 1], 1, "rounded_2"), PAIR))
-        h_tile(0, 768, BLOCK, "rounded_2")
-        add_shift(0, 768)
+        w1_q[1, 1].append(quantise("w1_1_1_1", rounded[1], PAIR))
+        h_tile(1, 0, HALF, "rounded_2")
+        h_tile(1, HALF, PAIR)
         scale_slots(1, 0, 0, 1)
+        add_pair(1, 0, 0, third_pair)
         scale_slots(1, 0, 256, 2)
-        h_tile(1, 0, HALF)
+        scale_slots(1, 0, 512, 4)
         scale_slots(1, 1, 0, 5)
-        add_shift(1, 0)
+        add_pair(1, 0, 1, third_pair)
         scale_slots(1, 1, 256, 6)
-        add_shift(1, 128, 0)
+        scale_slots(1, 1, 512, 1)
         add_shift(1, 256, 3)
         add_shift(1, 384, 7)
-        w3_q[0] = by_pairs(quantise("w3_0", round_weight(w3_raw[0], "rounded_4"), PASS))
-        pack_h(1, 0, HALF)
-        w3_q[1] = [quantise("w3_1_0", round_pair(w3_raw[1], 0, "rounded_1"), PAIR)]
-        pack_h(0, 768, BLOCK)
-        scale_slots(1, 0, 512, 5, "rounded_1")
-        w3_q[1].append(quantise("w3_1_1", round_pair(w3_raw[1], 1, "rounded_5"), PAIR))
-        h_tile(0, 896, BLOCK, "rounded_5")
-        add_shift(0, 896)
-        scale_slots(1, 1, 512, 0)
-        y_tile(0, HALF, "w1_raw_0_0")
-        decode(0, HALF, range(0, 1), 1)
-        store_y(0, HALF, range(0, 1))
-        decode(0, HALF, range(1, 2), 6)
-        store_y(0, HALF, range(1, 2))
-        decode(0, HALF, range(2, 3), 5)
-        decode(0, HALF, range(3, 4), 0)
-        store_y(0, HALF, range(2, 4))
-        h_tile(1, 512, PAIR)
-        scale_slots(1, 0, 768, 3, "scaled_0")
-        add_shift(1, 512, 4)
+        add_shift(1, 512, 0)
         add_shift(1, 640, 2)
+        w3_q[0] = by_pairs(quantise("w3_0", round_weight(w3_raw[0], "rounded_4"), PASS))
+        pack_h(1, HALF, PAIR)
+        pack_h(1, 0, HALF, "rounded_4")
+        rounded = round_pairs(w3_raw[1], ["rounded_1", "rounded_5"])
+        w3_q[1] = [quantise("w3_1_0", rounded[0], PAIR)]
+        scale_slots(1, 0, 768, 3)
+        w3_q[1].append(quantise("w3_1_1", rounded[1], PAIR))
         scale_slots(1, 1, 768, 7)
-        pack_h(1, 512, PAIR)
-        pack_h(0, 896, BLOCK)
+        y_tile(0, HALF, "w1_raw_0_0")
+        y_tile(HALF, HALF, "w1_raw_1_0")
+        decode(0, HALF, range(0, 1), 4)
+        store_y(0, HALF, range(0, 1))
+        decode(0, HALF, range(1, 2), 5)
+        store_y(0, HALF, range(1, 2))
+        decode(0, HALF, range(2, 3), 6)
+        store_y(0, HALF, range(2, 3))
+        decode(0, HALF, range(3, 4), 1)
+        store_y(0, HALF, range(3, 4))
         h_tile(1, 768, BLOCK)
         h_tile(1, 896, BLOCK)
-        add_shift(1, 768, 3)
-        add_shift(1, 896, 4)
-        rounded = [round_y(0, PAIR, nc.scalar.copy), round_y(256, BLOCK, nc.scalar.copy)]
-        y_tile(HALF, HALF, "w1_raw_0_1")
-        decode(512, PAIR, range(0, 2), 1)
+        add_shift(1, 768, 0)
+        add_shift(1, 896, 2)
+        decode(512, PAIR, range(0, 2), 4)
         store_y(512, PAIR, range(0, 2))
-        decode(512, PAIR, range(2, 4), 6)
+        decode(512, PAIR, range(2, 4), 5)
         store_y(512, PAIR, range(2, 4))
         pack_h(1, 768, BLOCK)
         pack_h(1, 896, BLOCK)
-        rounded.append(round_y(384, BLOCK, nc.vector.tensor_copy, "h_1_768"))
-        pack_y("h_1_896", *rounded)
-        decode(768, BLOCK, range(0, 4), 5)
-        decode(896, BLOCK, range(0, 4), 0, on_vector=True)
+        rounded = [round_y(0, PAIR, nc.vector.tensor_copy, "h_1_896"), round_y(256, PAIR, nc.vector.tensor_copy, "h_1_768")]
+        pack_y("y_codes_0", *rounded)
+        decode(768, PAIR, range(0, 2), 3)
+        decode(768, PAIR, range(2, 4), 7)
         store_y(768, PAIR, range(0, 4))
-        rounded = [round_y(512, BLOCK, nc.scalar.copy), round_y(640, BLOCK, nc.vector.tensor_copy)]
-        pack_y("y_codes_1", *rounded, round_y(768, BLOCK, nc.scalar.copy), round_y(896, BLOCK, nc.vector.tensor_copy))
+        rounded = [round_y(512, PAIR, nc.vector.tensor_copy), round_y(768, BLOCK, nc.scalar.copy)]
+        pack_y("y_codes_1", *rounded, round_y(896, BLOCK, nc.vector.tensor_copy))
 
         for q in range(4):
             queue = nc.scalar if q < 2 else nc.sync

@@ -157,7 +157,6 @@ def tile_list_style_modulated_decoder_kernel(
         w1_q = {}
         w3_q = {}
         scaled = {}
-        parked = {}
         h_rounded = {}
         h_q = {}
 
@@ -201,12 +200,20 @@ def tile_list_style_modulated_decoder_kernel(
             return b_bank[:].rearrange("p t c -> p c t")
 
         def park(place, g, lo, number):
-            parked[g, lo] = place
             nc.scalar.copy(place, shift_block(g, lo, number).rearrange("p c (u e) -> p u c e", e=2))
 
-        def add_pair(g, lo, u, shift):
+        sums = {}
+
+        def add_parked(g, lo, width, shift, u=slice(0, 2), buffer=None):
+            if (g, lo) not in sums:
+                sums[g, lo] = held(buffer or "sum_%d_%d" % (g, lo), [P, 2, width, 2], BF16)
+            nc.gpsimd.tensor_tensor(sums[g, lo][:, u], shift[:, u], scaled[g, lo][:, u, :width, :], ADD)
+
+        def weave(g, lo, width):
             tile, first = h_rounded[g, lo]
-            nc.gpsimd.tensor_tensor(tile[:, lo - first : lo - first + PAIR, u, :], shift[:, u], scaled[g, lo][:, u], ADD)
+            words = tile[:, lo - first : lo - first + width].rearrange("p c u e -> p (c u e)").bitcast(I32)
+            pairs = sums[g, lo][:].rearrange("p u c e -> p (u c e)").bitcast(I32)
+            nc.vector.tensor_copy(words.rearrange("p (c u) -> p c u", u=2), pairs.rearrange("p (u c) -> p c u", u=2))
 
         def h_tile(g, lo, width, buffer=None):
             tile = held(buffer or "h_%d_%d" % (g, lo), [P, width, 2, 2], BF16)
@@ -217,11 +224,8 @@ def tile_list_style_modulated_decoder_kernel(
             tile, first = h_rounded[g, lo]
             h_block = tile[:, lo - first : lo - first + BLOCK]
             scaled_block = scaled[g, lo][:, :, :BLOCK, :]
-            if (g, lo) in parked:
-                nc.gpsimd.tensor_tensor(h_block.rearrange("p c u e -> p u c e"), parked[g, lo], scaled_block, ADD)
-            else:
-                shift = shift_block(g, lo, number).rearrange("p c (u e) -> p c u e", e=2)
-                nc.vector.tensor_tensor(h_block, shift, scaled_block.rearrange("p u c e -> p c u e"), ADD)
+            shift = shift_block(g, lo, number).rearrange("p c (u e) -> p c u e", e=2)
+            nc.vector.tensor_tensor(h_block, shift, scaled_block.rearrange("p u c e -> p c u e"), ADD)
 
         def pack_h(g, lo, width, buffer=None):
             tile, first = h_rounded[g, lo]
@@ -329,35 +333,37 @@ def tile_list_style_modulated_decoder_kernel(
         h_tile(0, 0, HALF)
         h_tile(0, HALF, HALF)
         scale_slots(0, 0, 0, 0)
-        add_pair(0, 0, 0, first_pair)
+        add_parked(0, 0, PAIR, first_pair, 0)
         scale_slots(0, 0, 256, 1)
-        add_pair(0, 256, 0, second_pair)
+        add_parked(0, 256, PAIR, second_pair, 0)
         scale_slots(0, 0, 512, 2)
         scale_slots(0, 0, 768, 3)
         scale_slots(0, 1, 0, 7)
-        add_pair(0, 0, 1, first_pair)
+        add_parked(0, 0, PAIR, first_pair, 1)
         scale_slots(0, 1, 256, 0)
-        add_pair(0, 256, 1, second_pair)
+        add_parked(0, 256, PAIR, second_pair, 1)
         scale_slots(0, 1, 512, 3)
         scale_slots(0, 1, 768, 7)
         add_shift(0, 512, 0)
         add_shift(0, 640, 3)
         add_shift(0, 768, 7)
         add_shift(0, 896, 0)
-        pack_h(0, HALF, HALF)
         w1_q[0, 1] = by_pairs(quantise("w1_0_1", round_weight(w1_raw[0, 1], "rounded_0"), PASS))
+        weave(0, 0, PAIR)
+        weave(0, PAIR, PAIR)
         rounded = round_pairs(w1_raw[1, 1], ["rounded_3", "rounded_2"])
         w1_q[1, 1] = [quantise("w1_1_1_0", rounded[0], PAIR)]
-        pack_h(0, 0, HALF, "rounded_3")
+        pack_h(0, HALF, HALF, "rounded_0")
         w1_q[1, 1].append(quantise("w1_1_1_1", rounded[1], PAIR))
+        pack_h(0, 0, HALF, "rounded_3")
         h_tile(1, 0, HALF, "rounded_2")
         h_tile(1, HALF, PAIR)
         scale_slots(1, 0, 0, 1)
-        add_pair(1, 0, 0, third_pair)
+        add_parked(1, 0, PAIR, third_pair, 0)
         scale_slots(1, 0, 256, 2)
         scale_slots(1, 0, 512, 4)
         scale_slots(1, 1, 0, 5)
-        add_pair(1, 0, 1, third_pair)
+        add_parked(1, 0, PAIR, third_pair, 1)
         scale_slots(1, 1, 256, 6)
         scale_slots(1, 1, 512, 1)
         add_shift(1, 256, 3)
@@ -365,8 +371,9 @@ def tile_list_style_modulated_decoder_kernel(
         add_shift(1, 512, 0)
         add_shift(1, 640, 2)
         w3_q[0] = by_pairs(quantise("w3_0", round_weight(w3_raw[0], "rounded_4"), PASS))
+        weave(1, 0, PAIR)
         pack_h(1, HALF, PAIR)
-        pack_h(1, 0, HALF, "rounded_4")
+        pack_h(1, 0, HALF)
         rounded = round_pairs(w3_raw[1], ["rounded_1", "rounded_5"])
         w3_q[1] = [quantise("w3_1_0", rounded[0], PAIR)]
         scale_slots(1, 0, 768, 3)

@@ -106,12 +106,12 @@ def tile_list_style_modulated_decoder_kernel(
         load_x(0, [1], 0, S)
         w1_raw[0, 1] = load_w1(0, 1, pieces=2)
         w1_raw[1, 1] = load_w1(1, 1, pieces=2)
-        bias = held("bias", [P, SLOTS], F32)
-        nc.sync.dma_start(bias[:], b3.rearrange("(p t) -> p t", t=SLOTS))
         load_x(1, [0], 0, 3 * PAIR)
         load_x(1, [1], 0, 3 * PAIR)
         w3_raw = [load_weight("w3_raw_%d" % g, w3, g, 0, pieces=2) for g in range(2)]
         load_x(1, [0, 1], HALF + PAIR, S)
+        bias = held("bias", [P, SLOTS], F32)
+        nc.sync.dma_start(bias[:], b3.rearrange("(p t) -> p t", t=SLOTS))
 
         def gather(name, window, offsets, dtype, parts, buffer=None):
             width = S // parts
@@ -372,13 +372,13 @@ def tile_list_style_modulated_decoder_kernel(
         add_shift(1, 640, 2)
         w3_q[0] = by_pairs(quantise("w3_0", round_weight(w3_raw[0], "rounded_4"), PASS))
         weave(1, 0, PAIR)
-        pack_h(1, HALF, PAIR)
         pack_h(1, 0, HALF)
         rounded = round_pairs(w3_raw[1], ["rounded_1", "rounded_5"])
         w3_q[1] = [quantise("w3_1_0", rounded[0], PAIR)]
         scale_slots(1, 0, 768, 3)
         w3_q[1].append(quantise("w3_1_1", rounded[1], PAIR))
         scale_slots(1, 1, 768, 7)
+        pack_h(1, HALF, PAIR, "rounded_5")
         y_tile(0, HALF, "w1_raw_0_0")
         y_tile(HALF, HALF, "w1_raw_1_0")
         decode(0, HALF, range(0, 1), 4)
@@ -399,7 +399,7 @@ def tile_list_style_modulated_decoder_kernel(
         store_y(512, PAIR, range(2, 4))
         pack_h(1, 768, BLOCK)
         pack_h(1, 896, BLOCK)
-        rounded = [round_y(0, PAIR, nc.vector.tensor_copy, "h_1_896"), round_y(256, PAIR, nc.vector.tensor_copy, "h_1_768")]
+        rounded = [round_y(0, PAIR, nc.vector.tensor_copy, "h_1_768"), round_y(256, PAIR, nc.vector.tensor_copy, "h_1_896")]
         pack_y("y_codes_0", *rounded)
         decode(768, PAIR, range(0, 2), 3)
         decode(768, PAIR, range(2, 4), 7)
@@ -408,7 +408,6 @@ def tile_list_style_modulated_decoder_kernel(
         pack_y("y_codes_1", *rounded, round_y(896, BLOCK, nc.vector.tensor_copy))
 
         for q in range(4):
-            queue = nc.scalar if q < 2 else nc.sync
-            queue.dma_start(
+            nc.scalar.dma_start(
                 out_2[0, 4 * q : 4 * q + 4, :].bitcast(I32), y_plane[32 * q : 32 * q + 4, :].bitcast(I32)
             )

from contextlib import ExitStack

import concourse.mybir as mybir

K, K2, H, N, T, T2, S = 1024, 512, 1024, 512, 4096, 2048, 1024
FLOPS = 2 * S * (K * H + K2 * H + H * N)

F32 = mybir.dt.float32
BF16 = mybir.dt.bfloat16
I32 = mybir.dt.int32
U32 = mybir.dt.uint32
U16 = mybir.dt.uint16
U8 = mybir.dt.uint8
E4M3 = mybir.dt.float8_e4m3fn_x4
E2M1 = mybir.dt.float4_e2m1fn_x4
ADD = mybir.AluOpType.add
MULT = mybir.AluOpType.mult
IDENTITY = mybir.ActivationFunctionType.Identity

P = 128
SLOTS = 4
PASS = P * SLOTS
BANK = 512
BLOCK = BANK // SLOTS
PAIR = 2 * BLOCK
PAIRS = S // PAIR
HALF = S // 2
TAB_FIRST_ROW = 4


def tile_list_style_modulated_decoder_kernel(
    tc, tab_words, tab_scales, tab2_words, tab2_scales, offs, offs2, w1, w2_words, w2_scales, x, w3, b3,
    out_0, out_1, out_2,
):
    nc = tc.nc
    with ExitStack() as ctx:
        keep = ctx.enter_context(tc.tile_pool(name="keep", bufs=1))
        psum = ctx.enter_context(tc.psum_pool(name="psum", bufs=1))

        def held(name, shape, dtype):
            return keep.tile(shape, dtype, name=name, align_bytes=64)

        def bank(number, parts):
            return psum.tile([P, parts, BANK // parts], F32, name="bank_%d" % number)

        w2_plane_raw = held("w2_plane_raw", [P, H], U8)
        tab2_plane = held("tab2_plane", [P, T2], U8)
        tab_plane = held("tab_plane", [P, T], U8)
        for plane in (tab2_plane, tab_plane, w2_plane_raw):
            nc.vector.memset(plane[:].bitcast(I32), 0)

        for q in range(4):
            first = 32 * q + TAB_FIRST_ROW
            nc.gpsimd.dma_start(
                tab_plane[first : first + 8, :].bitcast(I32), tab_scales[:, 4 * q : 4 * q + 4, :].bitcast(I32)
            )

        def load_plane(plane, scales):
            for r in range(4):
                nc.sync.dma_start(plane[r:P:32, :].bitcast(I32), scales[0, r:16:4, :].bitcast(I32))

        def load_words(name, words, width):
            tile = held(name, [P, width], U32)
            nc.sync.dma_start(tile[:].bitcast(I32), words.rearrange("p n t -> p (n t)").bitcast(I32))
            return tile

        def load_rows(name, matrix, g, slots, lo, hi):
            tile = held(name, [P, len(slots), hi - lo], F32)
            by_slot = matrix[g * PASS : (g + 1) * PASS, lo:hi].rearrange("(p t) c -> p t c", t=SLOTS)
            nc.sync.dma_start(tile[:], by_slot[:, slots.start : slots.stop, :])
            return tile

        x_sb = {}

        def load_x(g, pairs, lo, hi):
            tile = load_rows("x_%d_%d_%d" % (g, pairs[0], lo), x, g, range(2 * pairs[0], 2 * pairs[-1] + 2), lo, hi)
            for k, u in enumerate(pairs):
                for at in range(lo, hi, BLOCK):
                    x_sb[g, u, at] = tile[:, 2 * k : 2 * k + 2, at - lo :]

        def load_weight(name, matrix, g, first, pieces=1):
            width = PASS // pieces
            return [
                load_rows(name + "_%d" % k * (k > 0), matrix, g, range(SLOTS), first + k * width, first + (k + 1) * width)
                for k in range(pieces)
            ]

        def load_w1(a, g, pieces=1):
            return load_weight("w1_raw_%d_%d" % (a, g), w1, a, g * PASS, pieces)

        w2_raw = held("w2_raw", [P, 2 * H], U8)
        nc.sync.dma_start(w2_raw[:].bitcast(I32), w2_words[0].bitcast(I32))
        list2 = held("list2", [P, S // 16], U16)
        nc.sync.dma_start(list2[:], offs2)
        tab2 = load_words("tab2", tab2_words[0], T2)
        load_plane(tab2_plane, tab2_scales)
        tab = [load_words("tab_0", tab_words[0], T)]
        list1 = held("list1", [P, S // 16], U16)
        nc.sync.dma_start(list1[:], offs)
        w1_raw = {}
        load_plane(w2_plane_raw, w2_scales)
        w1_raw[0, 0] = load_w1(0, 0)
        w1_raw[1, 0] = load_w1(1, 0)
        tab.append(load_words("tab_1", tab_words[1], T))
        load_x(0, [0], 0, S)
        load_x(0, [1], 0, S)
        w1_raw[0, 1] = load_w1(0, 1, pieces=2)
        w1_raw[1, 1] = load_w1(1, 1, pieces=2)
        load_x(1, [0], 0, 3 * PAIR)
        load_x(1, [1], 0, 3 * PAIR)
        w3_raw = [load_weight("w3_raw_%d" % g, w3, g, 0, pieces=2) for g in range(2)]
        load_x(1, [0, 1], HALF + PAIR, S)
        bias = held("bias", [P, SLOTS], F32)
        nc.sync.dma_start(bias[:], b3.rearrange("(p t) -> p t", t=SLOTS))

        def gather(name, window, offsets, dtype, parts, buffer=None):
            width = S // parts
            tiles = []
            for part in range(parts):
                picked = held(buffer or "%s_%d" % (name, part), [P, width], dtype)
                entries = offsets[:, part * width // 16 : (part + 1) * width // 16]
                nc.vector.tensor_copy(picked[:], window[:].indirect(entries))
                tiles.append(picked)
            return tiles

        def columns(tiles, lo, count, first_row=0):
            width = S // len(tiles)
            return tiles[lo // width][first_row:P, lo % width : lo % width + count]

        def round_weight(raw, buffer):
            dealt = held(buffer, [P, SLOTS * PASS], BF16)
            by_piece = dealt[:].rearrange("p (u e k m j) -> p k u m j e", u=2, e=2, k=len(raw), j=SLOTS)
            for k, piece in enumerate(raw):
                nc.scalar.copy(by_piece[:, k], piece[:].rearrange("p j (m u e) -> p u m j e", u=2, e=2))
            return dealt

        def round_pairs(raw, buffers):
            dealt = [held(buffer, [P, 2 * PASS], BF16) for buffer in buffers]
            for k, piece in enumerate(raw):
                for u in range(2):
                    nc.scalar.copy(
                        dealt[u][:].rearrange("p (e k m j) -> p k m j e", e=2, k=len(raw), j=SLOTS)[:, k],
                        piece[:].rearrange("p j (m u e) -> p u m j e", u=2, e=2)[:, u],
                    )
            return dealt

        def quantise(name, rounded, width, buffer=None):
            codes = held(buffer or name + "_codes", [P, width], U32)
            plane = held(name + "_plane", [P, width], U8)
            nc.vector.quantize_mx(codes[:].bitcast(E4M3), plane[:], rounded[:])
            return codes, plane

        def by_pairs(whole):
            codes, plane = whole
            return [(codes[:, u * PAIR : (u + 1) * PAIR], plane[:, u * PAIR : (u + 1) * PAIR]) for u in range(2)]

        w1_q = {}
        w3_q = {}
        scaled = {}
        h_rounded = {}
        h_q = {}

        def scale_slots(g, u, lo, number, buffer=None, width=PAIR):
            a_bank = psum.tile([P, 2, width], F32, name="bank_%d" % number)
            for a in range(2):
                codes, plane = w1_q[a, g][u]
                for e in range(2):
                    places = slice(e * P, (e + 1) * P)
                    nc.tensor.matmul_mx(
                        a_bank[:, e, :],
                        lhsT=codes[:, places].bitcast(E4M3),
                        lhsT_scale=plane[:, places],
                        rhs=columns(v_words[a], lo, width).bitcast(E4M3),
                        rhs_scale=columns(v_plane, lo, width, TAB_FIRST_ROW + 4 * a),
                        start=(a == 0 and e == 0),
                        stop=(a == 1 and e == 1),
                    )
            if u == 0:
                tile = held(buffer or "scaled_%d" % lo, [P, 2, width, 2], F32)
                for at in range(0, width, BLOCK):
                    scaled[g, lo + at] = tile[:, :, at:, :]
            nc.vector.scalar_tensor_tensor(
                scaled[g, lo][:, u], a_bank[:].rearrange("p e c -> p c e"), 1.0,
                x_sb[g, u, lo][:, :, :width].rearrange("p e c -> p c e"), ADD, MULT,
            )

        def shift_block(g, lo, number):
            b_bank = bank(number, SLOTS)
            for t in range(SLOTS):
                place = g * PASS + t * P
                nc.tensor.matmul_mx(
                    b_bank[:, t, :],
                    lhsT=w2_dealt[:, 2 * place : 2 * (place + P)].bitcast(E2M1),
                    lhsT_scale=w2_plane[:, place : place + P],
                    rhs=columns(v2_words, lo, BLOCK).bitcast(E4M3),
                    rhs_scale=columns(v2_plane, lo, BLOCK),
                    start=True,
                    stop=True,
                )
            return b_bank[:].rearrange("p t c -> p c t")

        def park(place, g, lo, number):
            nc.scalar.copy(place, shift_block(g, lo, number).rearrange("p c (u e) -> p u c e", e=2))

        sums = {}

        def add_parked(g, lo, width, shift, u=slice(0, 2), buffer=None):
            if (g, lo) not in sums:
                sums[g, lo] = held(buffer or "sum_%d_%d" % (g, lo), [P, 2, width, 2], BF16)
            nc.gpsimd.tensor_tensor(sums[g, lo][:, u], shift[:, u], scaled[g, lo][:, u, :width, :], ADD)

        def weave(g, lo, width):
            tile, first = h_rounded[g, lo]
            words = tile[:, lo - first : lo - first + width].rearrange("p c u e -> p (c u e)").bitcast(I32)
            pairs = sums[g, lo][:].rearrange("p u c e -> p (u c e)").bitcast(I32)
            nc.vector.tensor_copy(words.rearrange("p (c u) -> p c u", u=2), pairs.rearrange("p (u c) -> p c u", u=2))

        def h_tile(g, lo, width, buffer=None):
            tile = held(buffer or "h_%d_%d" % (g, lo), [P, width, 2, 2], BF16)
            for at in range(lo, lo + width, BLOCK):
                h_rounded[g, at] = (tile, lo)

        def add_shift(g, lo, number=None):
            tile, first = h_rounded[g, lo]
            h_block = tile[:, lo - first : lo - first + BLOCK]
            scaled_block = scaled[g, lo][:, :, :BLOCK, :]
            shift = shift_block(g, lo, number).rearrange("p c (u e) -> p c u e", e=2)
            nc.vector.tensor_tensor(h_block, shift, scaled_block.rearrange("p u c e -> p c u e"), ADD)

        def pack_h(g, lo, width, buffer=None):
            tile, first = h_rounded[g, lo]
            rounded = tile[:, lo - first : lo - first + width].rearrange("p c u e -> p (c u e)")
            codes, plane = quantise("h_%d_%d" % (g, lo), rounded, width, buffer)
            for at in range(lo, lo + width, BLOCK):
                h_q[g, at] = (codes, plane, lo, lo + width)

        out_rows = out_0.rearrange("(p t) j -> p t j", t=SLOTS)
        out_words = out_1[0].rearrange("p m t -> p (m t)").bitcast(I32)
        y_plane = held("y_plane", [P, S], U8)
        y_sb = {}

        def y_tile(lo, width, buffer):
            tile = held(buffer, [P, SLOTS, width], F32)
            for at in range(lo, lo + width, BLOCK):
                y_sb[at] = (tile, lo)

        def y_part(lo, width):
            tile, first = y_sb[lo]
            return tile[:, :, lo - first : lo - first + width]

        def decode(lo, width, slots, number, on_vector=False):
            y_bank = psum.tile([P, len(slots), width], F32, name="bank_%d" % number)
            passes = []
            for g in range(2):
                for e, t in enumerate(slots):
                    at = lo
                    while at < lo + width:
                        stop = min(h_q[g, at][3], lo + width)
                        passes.append((g, e, t, at, stop))
                        at = stop
            for k, (g, e, t, at, stop) in enumerate(passes):
                h_codes, h_plane, h_first = h_q[g, at][:3]
                codes, plane = w3_q[g][t // 2]
                places = slice(t % 2 * P, (t % 2 + 1) * P)
                nc.tensor.matmul_mx(
                    y_bank[:, e, at - lo : stop - lo],
                    lhsT=codes[:, places].bitcast(E4M3),
                    lhsT_scale=plane[:, places],
                    rhs=h_codes[:, at - h_first : stop - h_first].bitcast(E4M3),
                    rhs_scale=h_plane[:, at - h_first : stop - h_first],
                    start=(k == 0),
                    stop=(k == len(passes) - 1),
                )
            target = y_part(lo, width)
            if on_vector:
                spread = bias[:, slots.start : slots.stop].unsqueeze(2).to_broadcast([P, len(slots), width])
                nc.vector.tensor_tensor(target[:, slots.start : slots.stop, :], y_bank[:], spread, ADD)
            else:
                for e, t in enumerate(slots):
                    nc.scalar.activation(target[:, t, :], y_bank[:, e, :], IDENTITY, bias=bias[:, t : t + 1])

        def store_y(lo, width, slots):
            nc.sync.dma_start(
                out_rows[:, slots.start : slots.stop, lo : lo + width], y_part(lo, width)[:, slots.start : slots.stop, :]
            )

        def round_y(lo, width, copy, buffer=None):
            y_rounded = held(buffer or "y_rounded_%d" % lo, [P, SLOTS * width], BF16)
            copy(
                y_rounded[:].rearrange("p (c i t) -> p c t i", i=2, t=SLOTS),
                y_part(lo, width).rearrange("p t (c i) -> p c t i", i=2),
            )
            return lo, width, y_rounded

        def pack_y(buffer, *stretches):
            start = stretches[0][0]
            stop = stretches[-1][0] + stretches[-1][1]
            codes = held(buffer, [P, stop - start], U32)
            for lo, width, y_rounded in stretches:
                nc.vector.quantize_mx(
                    codes[:, lo - start : lo - start + width].bitcast(E4M3), y_plane[:, lo : lo + width], y_rounded[:]
                )
            nc.sync.dma_start(out_words[:, start:stop], codes[:].bitcast(I32))

        w2_dealt = held("w2_dealt", [P, 2 * H], U8)
        nc.vector.tensor_copy(
            w2_dealt[:].bitcast(U16).rearrange("p (g t m) -> p g t m", g=2, t=SLOTS),
            w2_raw[:].bitcast(U16).rearrange("p (g m t) -> p g t m", g=2, t=SLOTS),
        )
        v2_words = gather("v2_words", tab2, list2, U32, 1)
        v2_plane = gather("v2_plane", tab2_plane, list2, U8, 1)
        v_words = [gather("v_words_0", tab[0], list1, U32, 1)]
        w2_plane = held("w2_plane", [P, H], U8)
        nc.vector.tensor_copy(
            w2_plane[:].rearrange("p (g t m) -> p g t m", g=2, t=SLOTS),
            w2_plane_raw[:].rearrange("p (g m t) -> p g t m", g=2, t=SLOTS),
        )
        v_plane = gather("v_plane", tab_plane, list1, U8, 1, "w2_plane_raw")
        w1_q[0, 0] = by_pairs(quantise("w1_0_0", round_weight(w1_raw[0, 0], "rounded_0"), PASS))
        w1_q[1, 0] = by_pairs(quantise("w1_1_0", round_weight(w1_raw[1, 0], "rounded_1"), PASS))
        v_words.append(gather("v_words_1", tab[1], list1, U32, 2))
        first_pair = held("w1_raw_0_0", [P, 2, PAIR, 2], F32)
        park(first_pair[:, :, :BLOCK], 0, 0, 4)
        park(first_pair[:, :, BLOCK:], 0, 128, 5)
        parked_tile = held("w1_raw_1_0", [P, 2, 2, PAIR, 2], F32)
        second_pair = parked_tile[:, 0]
        park(second_pair[:, :, :BLOCK], 0, 256, 6)
        park(second_pair[:, :, BLOCK:], 0, 384, 7)
        third_pair = parked_tile[:, 1]
        park(third_pair[:, :, :BLOCK], 1, 0, 4)
        park(third_pair[:, :, BLOCK:], 1, 128, 5)

        h_tile(0, 0, HALF)
        h_tile(0, HALF, HALF)
        scale_slots(0, 0, 0, 0)
        add_parked(0, 0, PAIR, first_pair, 0)
        scale_slots(0, 0, 256, 1)
        add_parked(0, 256, PAIR, second_pair, 0)
        scale_slots(0, 0, 512, 2)
        scale_slots(0, 0, 768, 3)
        scale_slots(0, 1, 0, 7)
        add_parked(0, 0, PAIR, first_pair, 1)
        scale_slots(0, 1, 256, 0)
        add_parked(0, 256, PAIR, second_pair, 1)
        scale_slots(0, 1, 512, 3)
        scale_slots(0, 1, 768, 7)
        add_shift(0, 512, 0)
        add_shift(0, 640, 3)
        add_shift(0, 768, 7)
        add_shift(0, 896, 0)
        w1_q[0, 1] = by_pairs(quantise("w1_0_1", round_weight(w1_raw[0, 1], "rounded_0"), PASS))
        weave(0, 0, PAIR)
        weave(0, PAIR, PAIR)
        rounded = round_pairs(w1_raw[1, 1], ["rounded_3", "rounded_2"])
        w1_q[1, 1] = [quantise("w1_1_1_0", rounded[0], PAIR)]
        pack_h(0, HALF, HALF, "rounded_0")
        w1_q[1, 1].append(quantise("w1_1_1_1", rounded[1], PAIR))
        pack_h(0, 0, HALF, "rounded_3")
        h_tile(1, 0, HALF, "rounded_2")
        h_tile(1, HALF, PAIR)
        scale_slots(1, 0, 0, 1)
        add_parked(1, 0, PAIR, third_pair, 0)
        scale_slots(1, 0, 256, 2)
        scale_slots(1, 0, 512, 4)
        scale_slots(1, 1, 0, 5)
        add_parked(1, 0, PAIR, third_pair, 1)
        scale_slots(1, 1, 256, 6)
        scale_slots(1, 1, 512, 1)
        add_shift(1, 256, 3)
        add_shift(1, 384, 7)
        add_shift(1, 512, 0)
        add_shift(1, 640, 2)
        w3_q[0] = by_pairs(quantise("w3_0", round_weight(w3_raw[0], "rounded_4"), PASS))
        weave(1, 0, PAIR)
        pack_h(1, 0, HALF)
        rounded = round_pairs(w3_raw[1], ["rounded_1", "rounded_5"])
        w3_q[1] = [quantise("w3_1_0", rounded[0], PAIR)]
        scale_slots(1, 0, 768, 3)
        w3_q[1].append(quantise("w3_1_1", rounded[1], PAIR))
        scale_slots(1, 1, 768, 7)
        pack_h(1, HALF, PAIR, "rounded_5")
        y_tile(0, HALF, "w1_raw_0_0")
        y_tile(HALF, HALF, "w1_raw_1_0")
        decode(0, HALF, range(0, 1), 4)
        store_y(0, HALF, range(0, 1))
        decode(0, HALF, range(1, 2), 5)
        store_y(0, HALF, range(1, 2))
        decode(0, HALF, range(2, 3), 6)
        store_y(0, HALF, range(2, 3))
        decode(0, HALF, range(3, 4), 1)
        store_y(0, HALF, range(3, 4))
        h_tile(1, 768, BLOCK)
        h_tile(1, 896, BLOCK)
        add_shift(1, 768, 0)
        add_shift(1, 896, 2)
        decode(512, PAIR, range(0, 2), 4)
        store_y(512, PAIR, range(0, 2))
        decode(512, PAIR, range(2, 4), 5)
        store_y(512, PAIR, range(2, 4))
        pack_h(1, 768, BLOCK)
        pack_h(1, 896, BLOCK)
        rounded = [round_y(0, PAIR, nc.vector.tensor_copy, "h_1_768"), round_y(256, PAIR, nc.vector.tensor_copy, "h_1_896")]
        pack_y("y_codes_0", *rounded)
        decode(768, PAIR, range(0, 2), 3)
        decode(768, PAIR, range(2, 4), 7)
        store_y(768, PAIR, range(0, 4))
        rounded = [round_y(512, PAIR, nc.vector.tensor_copy), round_y(768, BLOCK, nc.scalar.copy)]
        pack_y("y_codes_1", *rounded, round_y(896, BLOCK, nc.vector.tensor_copy))

        for q in range(4):
            nc.scalar.dma_start(
                out_2[0, 4 * q : 4 * q + 4, :].bitcast(I32), y_plane[32 * q : 32 * q + 4, :].bitcast(I32)
            )
